import numpy as np, ml_dtypes
CORES = [23,119,17,113]
N = 4
BF = ml_dtypes.bfloat16
P, G, RO, C, J = 1024, 512, 3, 4, 2
W = P + (N - 1) * G
def parts(rng):
    w = rng.choice(np.array([4, 12, 40]), (N, 8, 1, 1))
    r = (120 * rng.random((N, 8, 1, P)) + w * rng.random((N, 8, 16, P))).astype(np.int64)
    v = (60 + 150 * rng.random((N, 8, 1, P)) + w * rng.random((N, 8, 16, P))).astype(np.int64)
    m = np.minimum(rng.poisson(0.4 + 0.35 * rng.random((N, 8, 1, 1, 16)), (N, 8, 16, 16, 16)), 15)
    low = rng.random((N, 8, 16, P)) < rng.choice(np.array([0.2, 0.5, 0.8]), (N, 8, 1, 1))
    s = np.where(low, rng.integers(0, G, low.shape), rng.integers(0, W, low.shape))
    return v, r, m, s
def pack(v, r, m, s):
    return {"v0": np.ascontiguousarray(v.reshape(N, 128, P)).astype(np.float32).astype(BF), "rew": np.ascontiguousarray(r.reshape(N, 128, P)).astype(np.float32).astype(BF),
            "mat": np.ascontiguousarray(m.reshape(N, 128, 256)).astype(np.float32).astype(BF), "succ": np.ascontiguousarray(s.reshape(N, 128, P)).astype(np.int32)}
def setup_inputs(rng):
    return pack(*parts(rng))
def near(rng, base):
    u = rng.integers(0, 4, (N, 8, 1, P)); i1 = rng.integers(0, 16, u.shape); i2 = (i1 + rng.integers(1, 16, u.shape)) % 16; st = np.arange(16)[:, None]
    return base + ((st == i1) & (u % 2 == 1)) - ((st == i2) & (u >= 2))
def setup_inputs_ties(rng):
    v, r, m, s = parts(rng); base = rng.integers(50, 201, (1, 8, 16, 1))
    r = near(rng, base); v = near(rng, base); m[:, :4] = 0; m[:, 4:6, :, 1::2] = 0; r[:, 4:] = r[:, 4:] >> 1
    return pack(v, r, m, s)
def setup_inputs_chains(rng):
    v, r, m, s = parts(rng); m[:, ::2] = 0
    o = np.argsort(rng.random((N, 8, P)), axis=-1); at = np.argsort(o, axis=-1)
    r = (at[:, :, None, :] + np.arange(16)[:, None]) >> 4; v = np.array(r)
    up = np.where(at == P - 1, rng.integers(P, W, at.shape), np.take_along_axis(o, np.minimum(at + 1, P - 1), 2)); down = np.take_along_axis(o, np.maximum(at - 1, 0), 2)
    v[0, ::4, :, :G] = P // 16 + 6
    for a in range(1, N): up[a, ::4] = np.where(at[a, ::4] == P - 1, P + (N - 1 - a) * G + up[a, ::4] % G, up[a, ::4])
    s[:, :, ::2] = up[:, :, None, :]
    s[:, 2::4, 0] = down[:, 2::4]; s[:, 3::4, 0] = down[:, 3::4]
    s[:, 2::4, 1::2] = rng.integers(G, W, s[:, 2::4, 1::2].shape)
    return pack(v, r, m, s)
def setup_inputs_alike(rng):
    v, r, m, s = parts(rng)
    s[:, 0] = rng.choice(np.array([0, P - 1, P, W - 1, G - 1, G]), (N, 16, P))
    s[:, 1] = np.arange(P)
    s[:, 2] = rng.integers(P, W, (N, 16, P))
    s[:, 3] = rng.integers(0, G, (N, 16, P))
    s[:, 4] = s[:, 4, :1]
    v[:, 5] = rng.integers(1, 200, (N, 1, 1))
    s[:, 6] = rng.integers(0, 8, (N, 16, P))
    return pack(v, r, m, s)
def setup_inputs_full(rng):
    v, r, m, s = parts(rng)
    r[:, 0] = 255
    r[:, 1] = 0; v[:, 1] = 0
    m[:, 2] = 15; v[:, 2] = rng.integers(0, 3, (N, 16, P))
    v[:, 3] = 0; v[rng.integers(0, N), 3] = 255
    v[:, 4] = 255 * rng.integers(0, 2, (N, 16, P)); r[:, 4] = rng.choice(np.array([0, 254, 255]), (N, 16, P))
    m[:, 5] = 0; m[:, 5, 0, :2] = 1; v[:, 5, 0] = rng.integers(126, 131, (N, P)); r[:, 5] = rng.integers(0, 2, (N, 16, P)); r[:, 5, 0] = rng.integers(126, 131, (N, P))
    m[:, 6] = 0; m[:, 6, :, 2] = rng.integers(13, 16, (N, 16, 16)); v[:, 6] = rng.integers(60, 241, (N, 1, P)) + rng.integers(0, 16, (N, 16, P)); r[:, 6] = rng.integers(0, 16, (N, 16, P))
    k = np.arange(16) != rng.integers(0, 16); h = rng.integers(0, 256, (N, 1, P))
    m[:, 7] = 0; m[:, 7, :, 1] = 15 * (k[:, None] == k[None, :]); v[:, 7] = np.where(k[:, None], h, 255 - h); r[:, 7] = rng.integers(0, 16, (N, 16, P))
    return pack(v, r, m, s)
def setup_inputs_spread(rng):
    v, r, m, s = parts(rng)
    v = np.minimum((np.exp2(8 * rng.random((N, 8, 1, P))) * rng.random((N, 8, 16, P))).astype(np.int64), 255)
    r = np.minimum((np.exp2(8 * rng.random((N, 8, 1, P))) * rng.random((N, 8, 16, P))).astype(np.int64), 255)
    m = np.minimum((16 * rng.random((N, 8, 16, 16, 16)) ** rng.choice(np.array([8, 16, 64]), (N, 8, 1, 1, 16))).astype(np.int64), 15)
    s = np.minimum((W * rng.random((N, 8, 16, P)) ** rng.choice(np.array([0.5, 1, 3]), (N, 8, 16, 1))).astype(np.int64), W - 1)
    return pack(v, r, m, s)
def check_inputs(d):
    bad = []
    for k, hi in (("v0", 255), ("rew", 255), ("mat", 15), ("succ", W - 1)):
        x = np.asarray(d[k]).astype(np.float64)
        if not (np.all(x >= 0) and np.all(x <= hi) and np.all(x == np.floor(x))): bad.append("whole numbers and range of " + k)
    return bad
def value(w, s, m, r):
    z = np.stack([m[g] @ np.take(w[g], s[g], axis=1).reshape(256, P) for g in range(8)])
    return np.minimum(255, r + np.floor(z * 2.0 ** -8))
def reference(v0, rew, mat, succ):
    v = v0.astype(np.float64).reshape(N, 8, 16, P); r = rew.astype(np.float64).reshape(N, 8, 16, P); s = succ.astype(np.int64).reshape(N, 8, 16, P)
    m = np.ascontiguousarray(mat.astype(np.float64).reshape(N, 8, 16, 16, 16).transpose(0, 1, 4, 2, 3)).reshape(N, 8, 16, 256)
    n = np.arange(P)
    for t in range(RO):
        nv, ns = [], []
        odd = ((np.arange(16) + t) & 1)[:, None] == 1
        for a in range(N):
            w = np.concatenate([v[a]] + [v[(a + d) % N][:, :, :G] for d in range(1, N)], axis=2)
            x = value(w, s[a], m[a], r[a])
            guest = (n + np.add.reduce(v[a], axis=1).astype(np.int64)) & (G - 1)
            e = np.take_along_axis(s[(a + t + 1) % N], guest[:, None, :], 2)
            c = np.where(odd, np.where(e < G, P + G * t + e, n), s[a])
            y = value(w, c, m[a], r[a])
            ok = np.all(y >= x, axis=1)[:, None, :]
            x = np.where(ok, y, x); c = np.where(ok, c, s[a])
            u = np.concatenate([x, w[:, :, P:]], axis=2); total = np.add.reduce(u, axis=1)
            D = np.tile(np.arange(W), (8, 1))
            for k in range(C - 1, -1, -1):
                h = c[:, 3 * k + t]
                good = np.all(np.take_along_axis(u, h[:, None, :], 2) >= x, axis=1) & (np.take_along_axis(total, h, 1) > total[:, :P])
                D[:, :P] = np.where(good, h, D[:, :P])
            for _ in range(J): D = np.take_along_axis(D, D, 1)
            nv.append(x); ns.append(np.take_along_axis(D, c.reshape(8, 16 * P), 1).reshape(8, 16, P))
        v = np.stack(nv); s = np.stack(ns)
    return {"yv": v.reshape(N, 128, P).astype(np.float32).astype(BF), "ys": s.reshape(N, 128, P).astype(np.float32)}

@@ -1,0 +1,520 @@
+from concourse.bass import DstId, RemoteDMATransfer
+from concourse.mybir import AluOpType as ALU, ActivationFunctionType as AF
+
+G2, G0, GH, G1, WE = 0, 1024, 2048, 3584, 4608
+GEN = [G0, G1, G2]
+OFF = [2816, 2816, 2048]
+CODE = [GH + 512 * t - OFF[t] for t in range(3)]
+BIG = 65536.0
+PRI = [8192.0 * (4 - k) - 16 * BIG for k in (0, 2, 1, 3)]
+RING = 16384
+YB = [(0, 2, 0, 512), (1, 3, 512, 896), (5, 7, 896, 1024)]
+FIN = [0, 512, 896, 1024]
+GATHER, PE, FIX, HOP = 1.5e-3, 0.5e-3, 0.12, 0.15
+PATIENCE, OWN = 0.4, 8.0
+
+SCRATCH = {}
+def _sb(names, n, d):
+    for x in names.split():
+        SCRATCH[x] = ("sbuf", [128, n], d)
+_sb("W0 W1 W2 E U", WE, "bfloat16")
+_sb("N1 N2", 2560, "bfloat16")
+_sb("rewb lt Gg", 1024, "bfloat16")
+_sb("GR", RING, "bfloat16")
+_sb("Ug sg", 4096, "bfloat16")
+_sb("Rcv0 Rcv1 Rcv2 Snd0 Snd1 Snd2 ones hi0 u0", 512, "bfloat16")
+_sb("BlkA BlkW Z0 Z01 Zbig Zpl Za Zb Zs1 Zs2 Zt1 Zt2 Ta0 Ta1 Ta2 Ta3 Ta4 Ta5", 144, "bfloat16")
+_sb("Ib Ip0 Ip1", 130, "bfloat16")
+_sb("Ch0 Ch1 BP BN Bp0 Bp1 Bn0 Bn1 Xm nXm Cst Ic Hm", 128, "bfloat16")
+_sb("fold", 256, "bfloat16")
+_sb("sc Ai", 1024, "int32")
+_sb("s16n B16", 1024, "float16")
+_sb("S0 S1 C16", 512, "float16")
+_sb("L0 L1 LB", 512, "uint16")
+_sb("LU", 256, "uint16")
+_sb("gl Dl Dp D2l La Lb", 64, "uint16")
+_sb("self0 self1 self2 selfb u32 s32", 512, "float32")
+_sb("outf", 1024, "float32")
+_sb("ckp PR uu", 256, "float32")
+_sb("CW dif tt1 Xf", 128, "float32")
+_sb("nw nb nok ns0 ns1 ns2 m0 m1", 64, "float32")
+_sb("gi gi2 mi mi2", 64, "int32")
+_sb("row16 oh cols gm", 16, "float32")
+_sb("pi", 4, "int32")
+SCRATCH["matb"] = ("sbuf", [128, 16, 16], "bfloat16")
+SCRATCH["Mbd"] = ("sbuf", [128, 16, 128], "bfloat16")
+for _b in range(8):
+    SCRATCH["P%d" % _b] = ("psum", [128, 512], "float32")
+
+SEMAPHORES = ["c_pe", "c_dve", "c_act", "c_pool"] + ["gh%d" % t for t in range(3)] + ["tp%d" % t for t in range(3)] \
+    + ["sg%d" % t for t in range(3)] + ["st%d" % t for t in range(3)] + ["d%d" % i for i in range(48)]
+
+
+def rank_program(g, core, T, topo):
+    rank = T.rank_of(core)
+    if rank is None:
+        return
+    NR = len(T.cores)
+    Q = {"pool": g, "pe": g.tensor, "dve": g.vector, "act": g.scalar, "sp": g.sync}
+    ops, hist, banks, prev, nd, ring, bias = [], {}, {}, {}, [0], [0], [0.0]
+
+    def R(name, lo=0, hi=None, step=1):
+        if hi is None:
+            hi = SCRATCH[name][1][1]
+        ap = T[name][:, lo:hi:step] if step > 1 else T[name][:, lo:hi]
+        return (ap, name, lo, hi, (hi - lo + step - 1) // step)
+
+    def rec(eng, fn, reads, writes, cost, lat=0.0, sem=None, cnt=0, gid=None, after=()):
+        i, deps = len(ops), set(after)
+        for rs, wr in ((reads, False), (writes, True)):
+            for r in rs:
+                name, lo, hi = r[1:4]
+                if name[0] == "P" and name[1:].isdigit():
+                    b = banks.setdefault(name, [[], []])
+                    deps.update(j for j in b[0] if j < i)
+                    if eng == "pe":
+                        deps.update(j for j in b[1] if j < i and (gid is None or ops[j]["gid"] != gid))
+                        b[1].append(i)
+                    else:
+                        deps.update(b[1])
+                        b[0], b[1] = [i], []
+                    continue
+                h = hist.setdefault(name, [])
+                deps.update(j for (l2, h2, j, w2) in h if j < i and l2 < hi and lo < h2 and (wr or w2))
+                if wr:
+                    h[:] = [e for e in h if not (lo <= e[0] and e[1] <= hi)]
+                h.append((lo, hi, i, wr))
+        order = [prev[eng]] if eng in prev else []
+        if eng in ("pool", "sp"):
+            prev[eng] = i
+        ops.append({"eng": eng, "fn": fn, "deps": deps, "order": order, "cost": cost, "lat": lat, "sem": sem, "cnt": cnt, "gid": gid, "bias": bias[0]})
+        return i
+
+    def num(x):
+        return x[0] if isinstance(x, tuple) else x
+
+    def aps(*xs):
+        return [x for x in xs if isinstance(x, tuple)]
+
+    def dur(out, a, rate=None):
+        if rate is None:
+            rate = 0.5 if all(SCRATCH[x[1]][2].endswith("16") for x in (out, a)) else 1
+        return FIX + max(64, rate * out[4]) * 1e-3
+
+    def ts(out, a, s1, op0, s2=None, op1=None):
+        if op1 is None:
+            rec("dve", lambda e: g.vector.tensor_scalar(out[0], a[0], num(s1), None, op0), aps(a, s1), [out], dur(out, a))
+        else:
+            rec("dve", lambda e: g.vector.tensor_scalar(out[0], a[0], num(s1), num(s2), op0, op1), aps(a, s1, s2), [out], dur(out, a))
+
+    def tt(out, a, b, op):
+        rec("dve", lambda e: g.vector.tensor_tensor(out[0], a[0], b[0], op), [a, b], [out], dur(out, a, 1 if SCRATCH[a[1]][0] == "psum" else 2))
+
+    def cp(out, a):
+        rec("dve", lambda e: g.vector.tensor_copy(out[0], a[0]), [a], [out], dur(out, a))
+
+    def cpa(out, a):
+        rec("any", lambda e: g.vector.tensor_copy(out[0], a[0]) if e == "dve" else g.scalar.activation(out[0], a[0], AF.Copy), [a], [out], dur(out, a, 1))
+
+    def ms(out, c):
+        rec("dve", lambda e: g.vector.memset(out[0], c), [], [out], dur(out, out))
+
+    def act(out, a, func, bias=None, scale=1.0):
+        if bias is None:
+            rec("act", lambda e: g.scalar.activation(out[0], a[0], func, scale=num(scale)), aps(a, scale), [out], dur(out, a, 1))
+        else:
+            rec("act", lambda e: g.scalar.activation(out[0], a[0], func, bias=bias[0]), [a, bias], [out], dur(out, a, 1))
+
+    def mm(calls, gid=None):
+        def fn(flags):
+            for k, (o, l, r) in enumerate(calls):
+                ins = g.tensor.matmul(o[0], l[0], r[0], flags[0] and k == 0, flags[1] and k == len(calls) - 1)
+            return ins
+        rec("pe", fn, [x for c in calls for x in c[1:]], [calls[0][0]], sum(max(64, c[2][4]) for c in calls) * PE, gid=gid)
+
+    def iota(out, pattern, base, cm):
+        if SCRATCH[out[1]][2] == "int32":
+            rec("pool", lambda e: g.iota(out[0], pattern, base, cm), [], [out], 0.13 + 2e-3 * out[4])
+        else:
+            rec("pool", lambda e: g.iota(out[0], pattern, base, cm, allow_small_or_imprecise_dtypes=True), [], [out], 0.13 + 2e-3 * out[4])
+
+    def sel(out, a, pattern, op, base, cm):
+        rec("pool", lambda e: g.affine_select(out[0], a[0], pattern, op, 0.0, base, cm), [a], [out], 0.17 + 2e-3 * out[4])
+
+    def dma(eng, out, in_, reads, writes, lat=2.5):
+        nd[0] += 1
+        rec(eng, lambda e: Q[eng].dma_start(out, in_), reads, writes, 0.1, lat, "d%d" % (nd[0] - 1), 16)
+
+    def copy(out, a):
+        dma("sp", out[0], a[0], [a], [out], 3.5)
+
+    def gat(out, win, off):
+        rec("any", lambda e: g.vector.tensor_copy(out[0], win[0].indirect(off[0])) if e == "dve"
+            else g.scalar.activation(out[0], win[0].indirect(off[0]), AF.Copy), [win, off], [out], 0.06 + GATHER * out[4])
+
+    def gat2(oname, o0, win, lname):
+        for hf in (0, 1):
+            gat(R(oname, o0 + 512 * hf, o0 + 512 * hf + 512), win, R(lname, 32 * hf, 32 * hf + 32))
+
+    def gring(win, lname, c0):
+        p = ring[0]
+        ring[0] = (p + 1024) % RING
+        gat(R("GR", p, p + 1024), win, R(lname, c0, c0 + 64))
+        return [R("GR", p + r, p + 1024, 16) for r in range(16)]
+
+    def Z(name, j):
+        return R(name, 16 - j, 144 - j)
+
+    def wrap(out, zname, src, lo):
+        mm([(out, Z(zname, j), R(src, lo + j, lo + 1024, 16)) for j in range(16)])
+
+    def turn(out, a, src):
+        mm([(out, Z("Ta%d" % a, 2 * j), R(src, j, 512, 8)) for j in range(8)])
+
+    def M(o):
+        return (T["Mbd"][:, o, :], "Mbd", 0, 16, 128)
+
+    def col(k):
+        return R("cols", k, k + 1)
+
+    def oh(k):
+        return R("oh", k, k + 1)
+
+    def P(b, lo=0, hi=512, step=1):
+        return R("P%d" % b, lo, hi, step)
+
+    def plan(src):
+        others = [c for c in T.cores if c != src]
+        far = [c for c in others if topo.chip(c) != topo.chip(src)]
+        out, used = {}, []
+        for i, c in enumerate(far):
+            e = topo.engines(src, c)
+            k = len(e) // len(far)
+            out[c] = e[i * k:(i + 1) * k]
+            used += e
+        for c in others:
+            if c not in out:
+                out[c] = [e for e in topo.engines(src, c) if e not in used][:4]
+        return out, sorted(set(used))
+
+    def bits(es):
+        return sum(1 << e for e in es)
+
+    def dst(c):
+        a = topo.addr(c)
+        return DstId(rid=a[0], pnc=a[1])
+
+    mine, wide = plan(core)
+
+    def send_ghosts(t, src):
+        trs = []
+        for d in range(1, NR):
+            c = T.cores[(rank - d) % NR]
+            trs.append(RemoteDMATransfer(dst_ids=[dst(c)], dma_engine_mask=bits(mine[c]), remote_sem=T.sem["gh%d" % t], src=src[0],
+                                         dst=T["W%d" % t][:, GH + 512 * (d - 1):GH + 512 * d]))
+        i = rec("pool", lambda e: g.remote_dma_fused(trs, local_sem=T.sem["sg%d" % t]), [src], [], 1.0, 7.0, "sg%d" % t,
+                sum(len(v) for v in mine.values()))
+        rec("ext", None, [], [R("W%d" % t, GH, G1)], 0.0, 0.0, "gh%d" % t, sum(len(plan(c)[0][core]) for c in T.cores if c != core), after=[i])
+
+    def send_tuples(t):
+        c = T.cores[(rank - t - 1) % NR]
+        tr = RemoteDMATransfer(dst_ids=[dst(c)], dma_engine_mask=bits(wide), remote_sem=T.sem["tp%d" % t], src=T["Snd%d" % t][:, :], dst=T["Rcv%d" % t][:, :])
+        i = rec("pool", lambda e: g.remote_dma_fused([tr], local_sem=T.sem["st%d" % t]), [R("Snd%d" % t)], [], 1.0, 8.0, "st%d" % t, len(wide))
+        rec("ext", None, [], [R("Rcv%d" % t)], 0.0, 0.0, "tp%d" % t, len(plan(T.cores[(rank + t + 1) % NR])[1]), after=[i])
+
+    bias[0] = 200.0
+    dma("sp", T.W0[:, G0:G0 + 512], T.v0[:, 0:512], [], [R("W0", G0, G0 + 512)], 3.0)
+    dma("act", T.sc[:, 0:512], T.succ[:, 0:512], [], [R("sc", 0, 512)], 4.0)
+    dma("sp", T.matb[:], T.mat[:, :], [], [R("matb")])
+    dma("act", T.sc[:, 512:1024], T.succ[:, 512:1024], [], [R("sc", 512, 1024)], 5.5)
+    dma("sp", T.W0[:, G0 + 512:GH], T.v0[:, 512:1024], [], [R("W0", G0 + 512, GH)], 4.0)
+    dma("sp", T.rewb[:, :], T.rew[:, :], [], [R("rewb")], 5.0)
+
+    ms(R("ones"), 1.0)
+    iota(R("pi", 0, 1), [[0, 1]], 0, 1)
+    iota(R("row16"), [[1, 16]], 0, 0)
+    sel(R("Ib"), R("ones", 0, 130), [[-1, 130]], ALU.is_equal, 1, 1)
+    sel(R("BlkA"), R("ones", 0, 144), [[-16, 9], [0, 16]], ALU.is_ge, 16, 1)
+    sel(R("BlkW"), R("BlkA"), [[16, 9], [0, 16]], ALU.is_ge, -1, -1)
+    send_ghosts(0, R("W0", G0, G0 + 512))
+    sel(R("Z0"), R("BlkW"), [[0, 9], [1, 16]], ALU.is_equal, 0, 0)
+    I, Blk = R("Ib", 1, 129), R("BlkW", 16, 144)
+    ms(R("W0", G2, G0), 0.0)
+    ts(R("pi", 1, 2), R("pi", 0, 1), 15, ALU.bitwise_and)
+    ts(R("pi", 2, 3), R("pi", 0, 1), 1, ALU.bitwise_and)
+    cp(R("cols", 0, 2), R("pi", 1, 3))
+    ts(col(2), col(1), -1.0, ALU.mult, 1.0, ALU.add)
+    ts(R("oh"), R("row16"), col(0), ALU.is_equal)
+    ts(R("Ip1"), R("Ib"), col(1), ALU.mult)
+    ts(R("Ip0"), R("Ib"), col(2), ALU.mult)
+    ts(col(11), col(2), 1024.0, ALU.mult)
+    ts(R("gm", 0, 8), R("BlkW", 16, 144, 16), 1.0 / 256, ALU.mult)
+    for t in range(3):
+        ts(col(8 + t), col(1), float(GEN[t] - OFF[t]), ALU.add)
+    ts(col(3), col(0), 2.0, ALU.is_lt)
+    tt(R("Hm"), R("Ip1", 2, 130), R("Ip1", 1, 129), ALU.subtract)
+    ts(col(4), oh(2), 2560.0, ALU.mult, col(3), ALU.add)
+    ts(col(5), oh(2), -1024.0, ALU.mult, col(3), ALU.add)
+    for t in (1, 2):
+        ts(col(11 + t), oh(3), 8192.0 if t == 1 else -8192.0, ALU.mult)
+        ts(col(5 + t), oh(2), float(CODE[t]), ALU.mult, col(11 + t), ALU.add)
+    for h in (0, 1):
+        tt(R("Ch%d" % h), R("Ip0", 1 - h, 129 - h), R("Ip1", 2 - h, 130 - h), ALU.add)
+    for k in range(4):
+        ms(R("PR", 64 * k, 64 * k + 64), PRI[k] + OFF[0])
+    ms(R("Cst"), (OFF[2] - OFF[0]) / 128.0)
+    act(R("Xf"), I, AF.Copy, scale=8191.0)
+    act(R("BP"), Blk, AF.Copy, scale=8192.0)
+    act(R("BN"), Blk, AF.Copy, scale=-8192.0)
+    act(R("Ic"), I, AF.Copy, scale=-1024.0)
+    for q in range(8):
+        rec("act", lambda e, q=q: g.scalar.activation(T.Mbd[:, :, 16 * q:16 * q + 16], T.matb[:], AF.Copy, scale=T.gm[:, q:q + 1]),
+            [R("matb"), R("gm")], [(None, "Mbd", q, q + 1)], 0.38)
+    tt(R("Xm"), R("Xf"), Blk, ALU.add)
+    iota(R("nb"), [[16, 64]], 0, 0)
+
+    def part(name, lo):
+        return (T[name][0:40, lo:lo + 64], name, lo, lo + 64, 64)
+
+    iota(part("fold", 0), [[0, 64]], 0, 64)
+    iota(part("fold", 64), [[1, 64]], 0, 0)
+    sel(part("fold", 128), part("ones", 0), [[0, 64]], ALU.is_ge, 15, -1)
+    sel(part("fold", 192), part("ones", 0), [[0, 64]], ALU.is_ge, -8, 1)
+    sel(R("Z01"), R("ones", 0, 144), [[0, 9], [-1, 16]], ALU.is_ge, 1, 0)
+    for a in (0, 3, 1, 4):
+        sel(R("Ta%d" % a), R("Z01"), [[-16, 9], [-1, 16]], ALU.is_equal, 16 - 2 * a, 1)
+    iota(R("selfb"), [[2, 512]], 0, 0)
+    for b in (0, 1):
+        ts(R("s16n", 512 * b, 512 * b + 512), R("sc", 512 * b, 512 * b + 512), float(G0 - OFF[0]), ALU.add)
+        for par in (1, 0):
+            mm([(P(6 + par, 256 * b, 256 * b + 256), R("Ip%d" % par, 1 + par - h, 129 + par - h), R("s16n", 512 * b + h, 512 * b + 512, 2)) for h in (0, 1)])
+    for par in (1, 0):
+        cp(R("S%d" % par), P(6 + par))
+        ts(R("L%d" % par), R("S%d" % par), float(OFF[0]), ALU.add)
+    ts(R("u0"), R("s16n", 0, 512), float(512 + G0 - OFF[0]), ALU.is_ge, -8192.0, ALU.mult)
+    mm([(P(4), I, R("s16n", 0, 512)), (P(4), I, R("u0"))])
+    act(R("hi0"), P(4), AF.Copy)
+    mm([(P(5), R("Ip1", 1, 129), R("s16n", 0, 512)), (P(5), R("Ip1", 1, 129), R("u0")), (P(5), R("Hm"), R("hi0"))])
+    act(R("Snd0"), P(5), AF.Identity, bias=col(11))
+    send_tuples(0)
+    for k in range(4):
+        dma("sp", T.E[k:k + 1, G0:G1], T.fold[0:40, 64 * k:64 * k + 64], [R("fold")], [(None, "rows", k, k + 1)])
+    for k in range(1, 4):
+        dma("sp", T.E[4 * k:4 * k + 4, G0:G1], T.E[0:4, G0:G1], [(None, "rows", 0, 4)], [(None, "rows", 10 + k, 11 + k)])
+    for k in range(1, 8):
+        dma("sp", T.E[16 * k:16 * k + 16, G0:G1], T.E[0:16, G0:G1], [(None, "rows", 0, 20)], [(None, "rows", 20 + k, 21 + k)])
+    done = (None, "rows", 0, 30)
+    dma("sp", T.E[:, G1:WE], T.E[:, G0:GH], [done], [R("E", G1, WE)])
+    dma("sp", T.E[:, G2:G0], T.E[:, G0:GH], [done], [R("E", G2, G0)])
+    dma("sp", T.N1[:, 1024:2560], T.E[:, GH:G1], [done], [R("N1", 1024, 2560)])
+    dma("sp", T.N2[:, 1024:2560], T.E[:, GH:G1], [done], [R("N2", 1024, 2560), R("E", G0, G1)])
+    for out in (R("U", G2, G0), R("W1", G2, G0), R("W2", G0, GH)):
+        copy(out, R("W0", G2, G0))
+    for h in (0, 1):
+        sel(R("Bp%d" % h), R("BP"), [[0, 64], [1, 2]], ALU.is_equal, -h, 0)
+        sel(R("Bn%d" % h), R("BN"), [[0, 64], [1, 2]], ALU.is_equal, -h, 0)
+    for a in (2, 5):
+        sel(R("Ta%d" % a), R("Z01"), [[-16, 9], [-1, 16]], ALU.is_equal, 16 - 2 * a, 1)
+    act(R("nw"), R("nb"), AF.Identity, bias=col(0))
+    act(R("Zbig"), R("Z0"), AF.Copy, scale=BIG)
+    act(R("nXm"), R("Xm"), AF.Copy, scale=-1.0)
+    for k, z in enumerate(("Zpl", "Za", "Zb", "Zt1", "Zt2")):
+        act(R(z), R("Z0"), AF.Copy, scale=col(3 + k))
+    for t in range(3):
+        act(R("self%d" % t), R("selfb"), AF.Identity, bias=col(8 + t))
+        ts(R("ns%d" % t), R("nw"), float(GEN[t]), ALU.add)
+    for t in (1, 2):
+        tt(R("Zs%d" % t), R("Zt%d" % t), R("Ta0"), ALU.add)
+
+    def guests(wname, gen, bank):
+        wrap(P(bank, 0, 64), "Z0", wname, gen)
+        tt(R("gi"), P(bank, 0, 64), R("nw"), ALU.add)
+        ts(R("gi2"), R("gi"), 511, ALU.bitwise_and)
+        cp(R("gl"), R("gi2"))
+
+    def compose(name, t):
+        if t == 2:
+            gat2(name, G1, R(name, 0, G1), "Lb")
+        gat2(name, G0, R(name, GH, WE), "La")
+
+    guests("W0", G0, 6)
+    bias[0] = 0.0
+    for t in range(3):
+        W, gen, ev, od = "W%d" % t, GEN[t], t % 2, (t + 1) % 2
+        Lo, Le, So = "L%d" % od, "L%d" % ev, R("S%d" % od)
+        top = G1 if t == 0 else WE
+        obs = [t, 6 + t, 3 + t, 9 + t]
+
+        def worth(lname, par, c0, to):
+            rows = gring(R(W, 0, top), lname, c0)
+            for bank in to:
+                mm([(P(bank, 2 * c0 % 512 + r % 2, 2 * c0 % 512 + 128, 2), M(2 * (r // 2) + par), rows[r]) for r in range(16)], (t, bank))
+
+        if t > 0:
+            for c0 in range(0, 256, 64):
+                rows = gring(R("E"), Lo, c0)
+                mm([(P(5, 2 * c0 + r % 2, 2 * c0 + 128, 2), Z("Zs%d" % t, 2 * (r // 2)), rows[r]) for r in range(16)], (t, "give"))
+            cpa(R("Snd%d" % t), P(5))
+            send_tuples(t)
+        copy(R("U", GH, G1), R(W, GH, G1))
+        for k in range(4):
+            turn(P(4, 64 * k, 64 * k + 64), obs[k] // 2, "S%d" % (obs[k] % 2))
+        tt(R("ckp"), P(4, 0, 256), R("PR"), ALU.add)
+        ts(R("LU", 0, 128), P(4, 0, 128), float(OFF[0]), ALU.add)
+        gat2("Gg", 0, R("Rcv%d" % t), "gl")
+        mm([(P(6), R("Ch%d" % h), R("Gg", h, 1024, 2)) for h in (0, 1)])
+        tt(R("C16"), P(6), R("self%d" % t), ALU.min if t == 1 else ALU.max)
+        ts(R("LB"), R("C16"), float(OFF[t]), ALU.add)
+        for k in (2, 3):
+            turn(P(6, 64 * k - 128, 64 * k - 64), obs[k] // 2, "C16")
+        for k in (0, 1):
+            ts(R("CW", 64 * k, 64 * k + 64), P(6, 64 * k, 64 * k + 64), OFF[t] + PRI[2 + k], ALU.add)
+        tt(R("dif"), R("ckp", 128, 256), R("CW"), ALU.subtract)
+        for b, (pa, pb, n0, n1) in enumerate(YB):
+            c = (n0, n1)
+            own, bank = [P(x, n0 % 512, (n1 - 1) % 512 + 1) for x in (pa, pb)]
+            mm([(own, I, R("rewb", *c))], (t, pa))
+            mm([(bank, I, R("rewb", *c))], (t, pb))
+            for c0 in range(n0 // 2, n1 // 2, 64):
+                worth(Lo, od, c0, [pa])
+                worth(Le, ev, c0, [pa, pb])
+            ts(R("Ai", *c), own, -255.0 / 512, ALU.add, 255.0, ALU.min)
+            for c0 in range(n0 // 2, n1 // 2, 64):
+                worth("LB", od, c0, [pb])
+            tt(R("lt", *c), bank, R("Ai", *c), ALU.is_lt)
+            ts(R("B16", *c), bank, 1024 - 255.0 / 512, ALU.add, 1279.0, ALU.min)
+            for l, r in ((R("Ic"), R("ones", 0, n1 - n0)), (R("BN"), R("lt", *c)), (I, R("B16", *c))):
+                mm([(own, l, r)], (t, "v", b))
+            tt(R("U", gen + n0, gen + n1), own, R("Ai", *c), ALU.max)
+        V = R("U", gen, gen + 1024)
+        if t < 2:
+            send_ghosts(t + 1, R("U", gen, gen + 512))
+            copy(R("W%d" % (t + 1), GEN[t + 1], GEN[t + 1] + 1024), V)
+        else:
+            dma("sp", T.yv[:, :], V[0], [V], [])
+        if t > 0:
+            compose("U", t)
+        wrap(P(4, 0, 64), "Zbig", "lt", 0)
+        ts(R("nok"), P(4, 0, 64), 1.0, ALU.min)
+        for k in (0, 1):
+            tt(R("tt1", 64 * k, 64 * k + 64), R("nok"), R("dif", 64 * k, 64 * k + 64), ALU.mult)
+        tt(R("ckp", 128, 256), R("tt1"), R("CW"), ALU.add)
+        for k in (2, 3):
+            ts(R("LU", 64 * k, 64 * k + 64), R("ckp", 64 * k, 64 * k + 64), -PRI[k], ALU.add)
+        for u in range(8):
+            bank, c = P(u % 4), (512 * u, 512 * u + 512)
+            gat(R("Ug", *c), R("U", 0, top), R("LU", 32 * u, 32 * u + 32))
+            mm([(bank, R("nXm"), R("U", gen + 512 * (u % 2), gen + 512 * (u % 2) + 512))], (t, "u", u))
+            mm([(bank, R("Xm"), R("Ug", *c))], (t, "u", u))
+            rec("any", lambda e, o=R("sg", *c)[0], a=bank[0]: g.vector.tensor_scalar(o, a, 0.0, None, ALU.is_gt) if e == "dve"
+                else g.scalar.activation(o, a, AF.Sign), [bank], [R("sg", *c)], FIX + 0.512)
+            if u % 2:
+                k = u // 2
+                wrap(P(4 + k, 0, 64), "Zbig", "sg", 1024 * k)
+                tt(R("uu", 64 * k, 64 * k + 64), P(4 + k, 0, 64), R("ckp", 64 * k, 64 * k + 64), ALU.add)
+                tt(R("mi") if k == 3 else R("m%d" % (k % 2)), R("uu", 64 * k, 64 * k + 64), R("ns%d" % t) if k == 0 else R("m%d" % ((k + 1) % 2)), ALU.max)
+        ts(R("mi2"), R("mi"), 8191, ALU.bitwise_and)
+        cp(R("Dl"), R("mi2"))
+        for sgn, bank in (("p", 0), ("n", 1)):
+            mm([(P(bank), I, R("C16"))] + [(P(bank), R("Cst"), R("ones"))] * (t == 2)
+               + [(P(bank), R("B%s%d" % (sgn, h)), R("lt", h, 1024, 2)) for h in (0, 1)])
+        tt(R("u32"), P(0), So, ALU.min)
+        tt(So if t < 2 else R("s32"), P(1), R("u32"), ALU.max)
+        ts(R(Lo), So if t < 2 else R("s32"), float(OFF[0]), ALU.add)
+        gat2("N1", 0, R("E"), "Dl")
+        if t == 0:
+            ts(R("Dp"), R("mi2"), float(-G0), ALU.add)
+        else:
+            wrap(P(4, 0, 64), "Zpl", "N1", 0)
+            cp(R("Dp"), P(4, 0, 64))
+        gat2("N2", 0, R("N1"), "Dp")
+        wrap(P(5, 0, 64), "Zpl", "N2", 0)
+        cp(R("D2l"), P(5, 0, 64))
+        gat2("E", gen, R("N2"), "D2l")
+        if t < 2:
+            wrap(P(4, 0, 64), "Za" if t == 0 else "Zb", "E", gen)
+            ts(R("La" if t == 0 else "Lb"), P(4, 0, 64), -1024.0 if t == 0 else 1024.0, ALU.add)
+            guests("U", gen, 2)
+            compose("W%d" % (t + 1), t + 1)
+        if t > 0:
+            compose("E", t)
+
+    for q in range(len(FIN) - 1):
+        n0, n1 = FIN[q], FIN[q + 1]
+        for par in (0, 1):
+            for c0 in range(n0 // 2, n1 // 2, 64):
+                rows = gring(R("E"), "L%d" % par, c0)
+                mm([(P(q, 2 * c0 - n0 + r % 2, 2 * c0 + 128 - n0, 2), Z("Zpl", 2 * (r // 2) + par), rows[r]) for r in range(16)], ("end", q))
+        cpa(R("outf", n0, n1), P(q, 0, n1 - n0))
+        dma("sp", T.ys[:, n0:n1], T.outf[:, n0:n1], [R("outf", n0, n1)], [])
+
+    n = len(ops)
+    users = [[] for _ in ops]
+    for i, o in enumerate(ops):
+        for j in set(o["deps"]) | set(o["order"]):
+            users[j].append(i)
+    rest = [0.0] * n
+    for i in range(n - 1, -1, -1):
+        rest[i] = ops[i]["cost"] + ops[i]["lat"] + HOP + max([rest[j] for j in users[i]] + [0.0]) + 1e-6 * (n - i)
+    rest = [r + o["bias"] for r, o in zip(rest, ops)]
+    left = [len(set(o["deps"]) | set(o["order"])) for o in ops]
+    ready, free, end, est, line = [i for i in range(n) if left[i] == 0], {}, [0.0] * n, [0.0] * n, []
+    while ready:
+        t0, e = min((max(free.get(x, 0.0), est[i]), x) for i in ready for x in (("act", "dve") if ops[i]["eng"] == "any" else (ops[i]["eng"],)))
+        mine_e = [i for i in ready if ops[i]["eng"] == e or (ops[i]["eng"] == "any" and e in ("act", "dve"))]
+        i = max((i for i in mine_e if est[i] <= t0), key=lambda i: rest[i] + (OWN if ops[i]["eng"] == e else 0))
+        soon = [j for j in mine_e if rest[j] > rest[i] and ops[j]["eng"] == e and est[j] - t0 < PATIENCE * ops[i]["cost"]]
+        if soon:
+            i = max(soon, key=lambda j: rest[j])
+        o = ops[i]
+        o["eng"] = e
+        free[e] = max(t0, est[i]) + o["cost"]
+        end[i] = free[e] + o["lat"]
+        ready.remove(i)
+        line.append(i)
+        for j in users[i]:
+            left[j] -= 1
+            if i in ops[j]["deps"]:
+                est[j] = max(est[j], end[i] + (0.0 if e == "pe" and ops[j]["eng"] == "pe" else HOP))
+            if left[j] == 0:
+                ready.append(j)
+
+    place = {i: k for k, i in enumerate(line)}
+    need, first, last = set(), {}, {}
+    for i in line:
+        o = ops[i]
+        latest = {}
+        for j in o["deps"]:
+            x = ops[j]["eng"]
+            if ops[j]["sem"] is None and not (x == "pe" and o["eng"] == "pe") and place[j] > place.get(latest.get(x), -1):
+                latest[x] = j
+        o["deps"] = [j for j in o["deps"] if ops[j]["sem"] is not None] + list(latest.values())
+        need.update(latest.values())
+        first.setdefault(o["gid"], i)
+        last[o["gid"]] = i
+    count, seen, final = {}, {}, {}
+    for i in line:
+        o = ops[i]
+        e = o["eng"]
+        if e != "ext":
+            for j in o["deps"]:
+                s, c = ops[j]["sem"], ops[j]["cnt"]
+                if seen.get((e, s), 0) < c:
+                    Q[e].wait_ge(T.sem[s], c)
+                    seen[(e, s)] = c
+            if e == "pe":
+                gid = o["gid"]
+                ins = o["fn"]((gid is None or first[gid] == i, gid is None or last[gid] == i))
+            else:
+                ins = o["fn"](e)
+            if o["sem"] is None and i in need:
+                count[e] = count.get(e, 0) + 1
+                o["sem"], o["cnt"] = "c_" + e, count[e]
+                ins.then_inc(T.sem[o["sem"]], 1)
+            elif o["sem"] is not None and e != "pool":
+                ins.then_inc(T.sem[o["sem"]], 16)
+        if o["sem"] is not None:
+            final[o["sem"]] = max(final.get(o["sem"], 0), o["cnt"])
+    for s in sorted(final):
+        if max([c for (e, s2), c in seen.items() if s2 == s] + [0]) < final[s]:
+            g.sync.wait_ge(T.sem[s], final[s])

@@ -1,43 +1,73 @@
 from concourse.bass import DstId, RemoteDMATransfer
 from concourse.mybir import AluOpType as ALU, ActivationFunctionType as AF
 
-G2, G0, GH, G1, WE = 0, 1024, 2048, 3584, 4608
-GEN = [G0, G1, G2]
-OFF = [2816, 2816, 2048]
-CODE = [GH + 512 * t - OFF[t] for t in range(3)]
+G0, GH, CU, PZ, WE = 0, 1024, 2560, 3584, 3600
+OFF = 1792
+HIGH = 2048.0
+LIFT = 1280.0
 BIG = 65536.0
-PRI = [8192.0 * (4 - k) - 16 * BIG for k in (0, 2, 1, 3)]
-RING = 16384
-YB = [(0, 2, 0, 512), (1, 3, 512, 896), (5, 7, 896, 1024)]
+MID = 128.0
+PRI = [8192.0 * (4 - k) + OFF for k in (0, 2, 1, 3)]
+RING = 24576
+YB = [0, 512, 896, 1024]
+YP = [(0, 1), (2, 5), (6, 7)]
+KA = [128, 96, 64]
+KB = [64, 64, 64]
+KG = [0, 64, 128, 176, 256]
+GC = [0, 256, 512]
+VC = [0, 512, 896, 1024]
+MED = [0, 512, 1024]
 FIN = [0, 512, 896, 1024]
-GATHER, PE, FIX, HOP = 1.5e-3, 0.5e-3, 0.12, 0.15
-PATIENCE, OWN = 0.4, 8.0
+KF = [128, 64, 64]
+DO = [0, 1, 3, 2]
+CYC = 0.83e-3
+GATHER = 1.3e-3
+PE = 0.43e-3
+FIX = 0.06
+HOP = 0.14
+ONCE = [0]
+REP = 1
+CK = [0, 2]
+RELAY = []
+FARG = [6.0, 7.0, 7.0]
+FART = [8.0, 5.0, 7.0]
+PATIENCE = 0.1
+OWN = 8.0
+QUICK = 6.0
+SHORT = 0.7
+URGENT = 20.0
+LAZY = -8.0
+STEP = 0.2
 
 SCRATCH = {}
 def _sb(names, n, d):
     for x in names.split():
         SCRATCH[x] = ("sbuf", [128, n], d)
-_sb("W0 W1 W2 E U", WE, "bfloat16")
-_sb("N1 N2", 2560, "bfloat16")
-_sb("rewb lt Gg", 1024, "bfloat16")
+_sb("W1 W2 E", PZ, "bfloat16")
+_sb("U", WE, "bfloat16")
+_sb("W0 N1 N2", CU, "bfloat16")
+_sb("rewb lt Gg EI", 1024, "bfloat16")
 _sb("GR", RING, "bfloat16")
-_sb("Ug sg", 4096, "bfloat16")
+_sb("Ug sg", 2048, "bfloat16")
+_sb("Um", 2048, "float16")
+_sb("mid", 1536, "bfloat16")
 _sb("Rcv0 Rcv1 Rcv2 Snd0 Snd1 Snd2 ones hi0 u0", 512, "bfloat16")
-_sb("BlkA BlkW Z0 Z01 Zbig Zpl Za Zb Zs1 Zs2 Zt1 Zt2 Ta0 Ta1 Ta2 Ta3 Ta4 Ta5", 144, "bfloat16")
+_sb("BlkA BlkW Z0 Z01 Zbig Zpl Za Zs1 Zs2 Ta0 Ta1 Ta2 Ta3 Ta4 Ta5", 144, "bfloat16")
 _sb("Ib Ip0 Ip1", 130, "bfloat16")
-_sb("Ch0 Ch1 BP BN Bp0 Bp1 Bn0 Bn1 Xm nXm Cst Ic Hm", 128, "bfloat16")
-_sb("fold", 256, "bfloat16")
+_sb("Ch0 Ch1 BP BN RW Bp0 Bp1 Bn0 Bn1 Rw0 Rw1 Xm nXm Ik Ih Is Ir Iw In won", 128, "bfloat16")
+_sb("fold zero PR", 256, "bfloat16")
 _sb("sc Ai", 1024, "int32")
-_sb("s16n B16", 1024, "float16")
-_sb("S0 S1 C16", 512, "float16")
+_sb("s16n A16 B16", 1024, "float16")
+_sb("ck", 256, "float16")
+_sb("S0 S1 C16 u16", 512, "float16")
+_sb("sv", 64, "float16")
 _sb("L0 L1 LB", 512, "uint16")
 _sb("LU", 256, "uint16")
-_sb("gl Dl Dp D2l La Lb", 64, "uint16")
-_sb("self0 self1 self2 selfb u32 s32", 512, "float32")
-_sb("outf", 1024, "float32")
-_sb("ckp PR uu", 256, "float32")
-_sb("CW dif tt1 Xf", 128, "float32")
-_sb("nw nb nok ns0 ns1 ns2 m0 m1", 64, "float32")
+_sb("gl Dl Dp D2l La", 64, "uint16")
+_sb("self0 self1 selfb", 512, "float32")
+_sb("outf Vh Xe", 1024, "float32")
+_sb("Xf", 128, "float32")
+_sb("nw nb nb0 nb1 ns0 ns1 m0 m1", 64, "float32")
 _sb("gi gi2 mi mi2", 64, "int32")
 _sb("row16 oh cols gm", 16, "float32")
 _sb("pi", 4, "int32")
@@ -46,7 +76,7 @@ SCRATCH["Mbd"] = ("sbuf", [128, 16, 128], "bfloat16")
 for _b in range(8):
     SCRATCH["P%d" % _b] = ("psum", [128, 512], "float32")
 
-SEMAPHORES = ["c_pe", "c_dve", "c_act", "c_pool"] + ["gh%d" % t for t in range(3)] + ["tp%d" % t for t in range(3)] \
+SEMAPHORES = ["c_pe", "c_dve", "c_act", "c_pool"] + [x + str(t) for x in ("sn", "gp") for t in range(3)] + ["gh%d" % t for t in range(3)] + ["tp%d" % t for t in range(3)] \
     + ["sg%d" % t for t in range(3)] + ["st%d" % t for t in range(3)] + ["d%d" % i for i in range(48)]
 
 
@@ -64,7 +94,7 @@ def rank_program(g, core, T, topo):
         ap = T[name][:, lo:hi:step] if step > 1 else T[name][:, lo:hi]
         return (ap, name, lo, hi, (hi - lo + step - 1) // step)
 
-    def rec(eng, fn, reads, writes, cost, lat=0.0, sem=None, cnt=0, gid=None, after=()):
+    def rec(eng, fn, reads, writes, cost, lat=0.0, sem=None, cnt=0, gid=None, after=(), fast=None):
         i, deps = len(ops), set(after)
         for rs, wr in ((reads, False), (writes, True)):
             for r in rs:
@@ -87,7 +117,8 @@ def rank_program(g, core, T, topo):
         order = [prev[eng]] if eng in prev else []
         if eng in ("pool", "sp"):
             prev[eng] = i
-        ops.append({"eng": eng, "fn": fn, "deps": deps, "order": order, "cost": cost, "lat": lat, "sem": sem, "cnt": cnt, "gid": gid, "bias": bias[0]})
+        ops.append({"eng": eng, "fn": fn, "deps": deps, "order": order, "cost": cost, "lat": lat, "sem": sem, "cnt": cnt, "gid": gid, "bias": bias[0],
+                    "fast": fast or cost})
         return i
 
     def num(x):
@@ -99,7 +130,7 @@ def rank_program(g, core, T, topo):
     def dur(out, a, rate=None):
         if rate is None:
             rate = 0.5 if all(SCRATCH[x[1]][2].endswith("16") for x in (out, a)) else 1
-        return FIX + max(64, rate * out[4]) * 1e-3
+        return FIX + max(64, rate * out[4]) * CYC
 
     def ts(out, a, s1, op0, s2=None, op1=None):
         if op1 is None:
@@ -113,17 +144,23 @@ def rank_program(g, core, T, topo):
     def cp(out, a):
         rec("dve", lambda e: g.vector.tensor_copy(out[0], a[0]), [a], [out], dur(out, a))
 
-    def cpa(out, a):
-        rec("any", lambda e: g.vector.tensor_copy(out[0], a[0]) if e == "dve" else g.scalar.activation(out[0], a[0], AF.Copy), [a], [out], dur(out, a, 1))
-
     def ms(out, c):
         rec("dve", lambda e: g.vector.memset(out[0], c), [], [out], dur(out, out))
 
-    def act(out, a, func, bias=None, scale=1.0):
-        if bias is None:
-            rec("act", lambda e: g.scalar.activation(out[0], a[0], func, scale=num(scale)), aps(a, scale), [out], dur(out, a, 1))
-        else:
-            rec("act", lambda e: g.scalar.activation(out[0], a[0], func, bias=bias[0]), [a, bias], [out], dur(out, a, 1))
+    def either(out, a, func, op, s):
+        def fn(e):
+            if e == "dve":
+                return g.vector.tensor_scalar(out[0], a[0], num(s), None, op)
+            if op == ALU.add:
+                return g.scalar.activation(out[0], a[0], func, bias=num(s))
+            return g.scalar.activation(out[0], a[0], func, scale=num(s) if op == ALU.mult else 1.0)
+        rec("any", fn, aps(a, s), [out], dur(out, a, 1), fast=dur(out, a))
+
+    def scl(out, a, s):
+        either(out, a, AF.Copy, ALU.mult, s)
+
+    def shift(out, a, s):
+        either(out, a, AF.Identity, ALU.add, s)
 
     def mm(calls, gid=None):
         def fn(flags):
@@ -134,45 +171,62 @@ def rank_program(g, core, T, topo):
 
     def iota(out, pattern, base, cm):
         if SCRATCH[out[1]][2] == "int32":
-            rec("pool", lambda e: g.iota(out[0], pattern, base, cm), [], [out], 0.13 + 2e-3 * out[4])
+            rec("pool", lambda e: g.iota(out[0], pattern, base, cm), [], [out], 0.13 + 2 * CYC * out[4])
         else:
-            rec("pool", lambda e: g.iota(out[0], pattern, base, cm, allow_small_or_imprecise_dtypes=True), [], [out], 0.13 + 2e-3 * out[4])
+            rec("pool", lambda e: g.iota(out[0], pattern, base, cm, allow_small_or_imprecise_dtypes=True), [], [out], 0.13 + 2 * CYC * out[4])
 
     def sel(out, a, pattern, op, base, cm):
-        rec("pool", lambda e: g.affine_select(out[0], a[0], pattern, op, 0.0, base, cm), [a], [out], 0.17 + 2e-3 * out[4])
+        rec("pool", lambda e: g.affine_select(out[0], a[0], pattern, op, 0.0, base, cm), [a], [out], 0.17 + 2 * CYC * out[4])
 
-    def dma(eng, out, in_, reads, writes, lat=2.5):
+    def dma(eng, out, in_, reads, writes, lat=2.5, after=()):
         nd[0] += 1
-        rec(eng, lambda e: Q[eng].dma_start(out, in_), reads, writes, 0.1, lat, "d%d" % (nd[0] - 1), 16)
+        rec(eng, lambda e: g.dma_start(out, in_, accum_op=ALU.add) if eng == "pool" else Q[eng].dma_start(out, in_), reads, writes, 0.1, lat,
+            "d%d" % (nd[0] - 1), 16, after=after)
 
-    def copy(out, a):
-        dma("sp", out[0], a[0], [a], [out], 3.5)
+    def old_ghosts(t):
+        u = R("U", GH, CU)
+        dma("pool", u[0], T["W%d" % t][:, GH:CU], [R("W%d" % t, GH, CU), u], [u], 4.0)
 
-    def gat(out, win, off):
-        rec("any", lambda e: g.vector.tensor_copy(out[0], win[0].indirect(off[0])) if e == "dve"
-            else g.scalar.activation(out[0], win[0].indirect(off[0]), AF.Copy), [win, off], [out], 0.06 + GATHER * out[4])
+    def copy(out, a, after=()):
+        dma("sp", out[0], a[0], [a], [out], 3.0, after)
+
+    def gat(out, win, off, eng="any"):
+        rec(eng, lambda e: g.vector.tensor_copy(out[0], win[0].indirect(off[0])) if e == "dve"
+            else g.scalar.activation(out[0], win[0].indirect(off[0]), AF.Copy), [win, off], [out], FIX + GATHER * out[4])
+
+    def least(out, win, off, old):
+        rec("dve", lambda e: g.vector.tensor_tensor(out[0], win[0].indirect(off[0]), old[0], ALU.min), [win, off, old], [out], FIX + GATHER * out[4])
 
     def gat2(oname, o0, win, lname):
         for hf in (0, 1):
             gat(R(oname, o0 + 512 * hf, o0 + 512 * hf + 512), win, R(lname, 32 * hf, 32 * hf + 32))
 
-    def gring(win, lname, c0):
-        p = ring[0]
-        ring[0] = (p + 1024) % RING
-        gat(R("GR", p, p + 1024), win, R(lname, c0, c0 + 64))
-        return [R("GR", p + r, p + 1024, 16) for r in range(16)]
+    def slot(k):
+        if ring[0] + 16 * k > RING:
+            ring[0] = 0
+        ring[0] += 16 * k
+        return R("GR", ring[0] - 16 * k, ring[0])
+
+    def rows(x):
+        return [R(x[1], x[2] + r, x[3], 16) for r in range(16)]
+
+    def units(n0, n1, k):
+        return [(c0, min(c0 + k, n1 // 2)) for c0 in range(n0 // 2, n1 // 2, k)]
+
+    def fold16(bank, base, c, mats, x, gid):
+        mm([(P(bank, 2 * c[0] - base + r % 2, 2 * c[1] - base, 2), mats(r // 2), v) for r, v in enumerate(rows(x))], gid)
 
     def Z(name, j):
         return R(name, 16 - j, 144 - j)
 
-    def wrap(out, zname, src, lo):
-        mm([(out, Z(zname, j), R(src, lo + j, lo + 1024, 16)) for j in range(16)])
+    def wrap(out, zname, src, lo, gid=None):
+        mm([(out, Z(zname, j), R(src, lo + j, lo + 1024, 16)) for j in range(16)], gid)
 
-    def turn(out, a, src):
-        mm([(out, Z("Ta%d" % a, 2 * j), R(src, j, 512, 8)) for j in range(8)])
+    def turn(out, a, src, gid=None):
+        mm([(out, Z("Ta%d" % a, 2 * j), R(src, j, 512, 8)) for j in range(8)], gid)
 
-    def M(o):
-        return (T["Mbd"][:, o, :], "Mbd", 0, 16, 128)
+    def M(o, name="Mbd"):
+        return (T[name][:, o, :], name, 0, 16, 128)
 
     def col(k):
         return R("cols", k, k + 1)
@@ -182,6 +236,9 @@ def rank_program(g, core, T, topo):
 
     def P(b, lo=0, hi=512, step=1):
         return R("P%d" % b, lo, hi, step)
+
+    def ones(n):
+        return R("ones", 0, n)
 
     def plan(src):
         others = [c for c in T.cores if c != src]
@@ -194,7 +251,7 @@ def rank_program(g, core, T, topo):
             used += e
         for c in others:
             if c not in out:
-                out[c] = [e for e in topo.engines(src, c) if e not in used][:4]
+                out[c] = [e for e in topo.engines(src, c) if e not in used][::2]
         return out, sorted(set(used))
 
     def bits(es):
@@ -205,247 +262,325 @@ def rank_program(g, core, T, topo):
         return DstId(rid=a[0], pnc=a[1])
 
     mine, wide = plan(core)
+    near = [c for c in mine if topo.chip(c) == topo.chip(core)][0]
+    twin = [c for c in mine if c != near and topo.die(c) == topo.die(core)][0]
 
     def send_ghosts(t, src):
-        trs = []
-        for d in range(1, NR):
-            c = T.cores[(rank - d) % NR]
-            trs.append(RemoteDMATransfer(dst_ids=[dst(c)], dma_engine_mask=bits(mine[c]), remote_sem=T.sem["gh%d" % t], src=src[0],
-                                         dst=T["W%d" % t][:, GH + 512 * (d - 1):GH + 512 * d]))
-        i = rec("pool", lambda e: g.remote_dma_fused(trs, local_sem=T.sem["sg%d" % t]), [src], [], 1.0, 7.0, "sg%d" % t,
-                sum(len(v) for v in mine.values()))
-        rec("ext", None, [], [R("W%d" % t, GH, G1)], 0.0, 0.0, "gh%d" % t, sum(len(plan(c)[0][core]) for c in T.cores if c != core), after=[i])
+        W = "W%d" % t
+
+        def place(of, at):
+            d = (T.rank_of(of) - T.rank_of(at)) % NR
+            return R(W, GH + 512 * (d - 1), GH + 512 * d)
+
+        def write(a, of, part, lsem, lat):
+            trs = [RemoteDMATransfer(dst_ids=[dst(c)], dma_engine_mask=bits(es), remote_sem=T.sem[sem], src=a[0], dst=place(of, c)[0]) for c, es, sem in part]
+            return rec("pool", lambda e: g.remote_dma_fused(trs, local_sem=T.sem[lsem]), [a], [], 0.7, lat, lsem, sum(len(es) for c, es, sem in part))
+
+        if t in RELAY:
+            i = write(src, core, [(twin, wide, "gp%d" % t), (near, mine[near], "gh%d" % t)], "sg%d" % t, FARG[t])
+            rec("ext", None, [], [place(twin, core)], 0.0, 0.0, "gp%d" % t, len(wide), after=[i])
+            j = write(place(twin, core), twin, [(near, mine[near], "gh%d" % t)], "sn%d" % t, 4.0)
+            rec("ext", None, [], [place(c, core) for c in mine if c != twin], 0.0, 0.0, "gh%d" % t, 2 * len(mine[near]), after=[j])
+        else:
+            i = write(src, core, [(c, mine[c], "gh%d" % t) for c in mine], "sg%d" % t, FARG[t])
+            rec("ext", None, [], [R(W, GH, CU)], 0.0, 0.0, "gh%d" % t, sum(len(plan(c)[0][core]) for c in mine), after=[i])
+        return i
 
     def send_tuples(t):
         c = T.cores[(rank - t - 1) % NR]
         tr = RemoteDMATransfer(dst_ids=[dst(c)], dma_engine_mask=bits(wide), remote_sem=T.sem["tp%d" % t], src=T["Snd%d" % t][:, :], dst=T["Rcv%d" % t][:, :])
-        i = rec("pool", lambda e: g.remote_dma_fused([tr], local_sem=T.sem["st%d" % t]), [R("Snd%d" % t)], [], 1.0, 8.0, "st%d" % t, len(wide))
+        i = rec("pool", lambda e: g.remote_dma_fused([tr], local_sem=T.sem["st%d" % t]), [R("Snd%d" % t)], [], 1.0, FART[t], "st%d" % t, len(wide))
         rec("ext", None, [], [R("Rcv%d" % t)], 0.0, 0.0, "tp%d" % t, len(plan(T.cores[(rank + t + 1) % NR])[1]), after=[i])
+        return i
 
     bias[0] = 200.0
-    dma("sp", T.W0[:, G0:G0 + 512], T.v0[:, 0:512], [], [R("W0", G0, G0 + 512)], 3.0)
-    dma("act", T.sc[:, 0:512], T.succ[:, 0:512], [], [R("sc", 0, 512)], 4.0)
-    dma("sp", T.matb[:], T.mat[:, :], [], [R("matb")])
-    dma("act", T.sc[:, 512:1024], T.succ[:, 512:1024], [], [R("sc", 512, 1024)], 5.5)
-    dma("sp", T.W0[:, G0 + 512:GH], T.v0[:, 512:1024], [], [R("W0", G0 + 512, GH)], 4.0)
-    dma("sp", T.rewb[:, :], T.rew[:, :], [], [R("rewb")], 5.0)
+    dma("sp", T.W0[:, G0:G0 + 512], T.v0[:, 0:512], [], [R("W0", G0, G0 + 512)], 2.2)
+    dma("act", T.sc[:, 0:512], T.succ[:, 0:512], [], [R("sc", 0, 512)], 3.0)
+    dma("sp", T.matb[:], T.mat[:, :], [], [R("matb")], 3.2)
+    dma("act", T.sc[:, 512:1024], T.succ[:, 512:1024], [], [R("sc", 512, 1024)], 4.2)
+    dma("sp", T.W0[:, G0 + 512:GH], T.v0[:, 512:1024], [], [R("W0", G0 + 512, GH)], 4.5)
+    dma("sp", T.rewb[:, :], T.rew[:, :], [], [R("rewb")], 5.5)
 
-    ms(R("ones"), 1.0)
+    ms(ones(512), 1.0)
     iota(R("pi", 0, 1), [[0, 1]], 0, 1)
     iota(R("row16"), [[1, 16]], 0, 0)
-    sel(R("Ib"), R("ones", 0, 130), [[-1, 130]], ALU.is_equal, 1, 1)
-    sel(R("BlkA"), R("ones", 0, 144), [[-16, 9], [0, 16]], ALU.is_ge, 16, 1)
+    sel(R("Ib"), ones(130), [[-1, 130]], ALU.is_equal, 1, 1)
+    sel(R("BlkA"), ones(144), [[-16, 9], [0, 16]], ALU.is_ge, 16, 1)
     sel(R("BlkW"), R("BlkA"), [[16, 9], [0, 16]], ALU.is_ge, -1, -1)
     send_ghosts(0, R("W0", G0, G0 + 512))
     sel(R("Z0"), R("BlkW"), [[0, 9], [1, 16]], ALU.is_equal, 0, 0)
+    iota(R("nb"), [[16, 64]], int(16 * MID), 0)
+    iota(R("selfb"), [[2, 512]], 0, 0)
+    iota(R("nb0"), [[16, 64]], int(16 * BIG) + G0, 0)
+    iota(R("nb1"), [[16, 64]], int(16 * BIG) + CU, 0)
     I, Blk = R("Ib", 1, 129), R("BlkW", 16, 144)
-    ms(R("W0", G2, G0), 0.0)
     ts(R("pi", 1, 2), R("pi", 0, 1), 15, ALU.bitwise_and)
     ts(R("pi", 2, 3), R("pi", 0, 1), 1, ALU.bitwise_and)
     cp(R("cols", 0, 2), R("pi", 1, 3))
     ts(col(2), col(1), -1.0, ALU.mult, 1.0, ALU.add)
-    ts(R("oh"), R("row16"), col(0), ALU.is_equal)
-    ts(R("Ip1"), R("Ib"), col(1), ALU.mult)
-    ts(R("Ip0"), R("Ib"), col(2), ALU.mult)
-    ts(col(11), col(2), 1024.0, ALU.mult)
-    ts(R("gm", 0, 8), R("BlkW", 16, 144, 16), 1.0 / 256, ALU.mult)
-    for t in range(3):
-        ts(col(8 + t), col(1), float(GEN[t] - OFF[t]), ALU.add)
-    ts(col(3), col(0), 2.0, ALU.is_lt)
-    tt(R("Hm"), R("Ip1", 2, 130), R("Ip1", 1, 129), ALU.subtract)
-    ts(col(4), oh(2), 2560.0, ALU.mult, col(3), ALU.add)
-    ts(col(5), oh(2), -1024.0, ALU.mult, col(3), ALU.add)
-    for t in (1, 2):
-        ts(col(11 + t), oh(3), 8192.0 if t == 1 else -8192.0, ALU.mult)
-        ts(col(5 + t), oh(2), float(CODE[t]), ALU.mult, col(11 + t), ALU.add)
-    for h in (0, 1):
-        tt(R("Ch%d" % h), R("Ip0", 1 - h, 129 - h), R("Ip1", 2 - h, 130 - h), ALU.add)
-    for k in range(4):
-        ms(R("PR", 64 * k, 64 * k + 64), PRI[k] + OFF[0])
-    ms(R("Cst"), (OFF[2] - OFF[0]) / 128.0)
-    act(R("Xf"), I, AF.Copy, scale=8191.0)
-    act(R("BP"), Blk, AF.Copy, scale=8192.0)
-    act(R("BN"), Blk, AF.Copy, scale=-8192.0)
-    act(R("Ic"), I, AF.Copy, scale=-1024.0)
+    scl(R("Ip1"), R("Ib"), col(1))
+    scl(R("Ip0"), R("Ib"), col(2))
+    scl(col(11), col(2), -1024.0)
+    scl(R("gm", 0, 8), R("BlkW", 16, 144, 16), 1.0 / 256)
     for q in range(8):
-        rec("act", lambda e, q=q: g.scalar.activation(T.Mbd[:, :, 16 * q:16 * q + 16], T.matb[:], AF.Copy, scale=T.gm[:, q:q + 1]),
-            [R("matb"), R("gm")], [(None, "Mbd", q, q + 1)], 0.38)
-    tt(R("Xm"), R("Xf"), Blk, ALU.add)
-    iota(R("nb"), [[16, 64]], 0, 0)
-
-    def part(name, lo):
-        return (T[name][0:40, lo:lo + 64], name, lo, lo + 64, 64)
-
-    iota(part("fold", 0), [[0, 64]], 0, 64)
-    iota(part("fold", 64), [[1, 64]], 0, 0)
-    sel(part("fold", 128), part("ones", 0), [[0, 64]], ALU.is_ge, 15, -1)
-    sel(part("fold", 192), part("ones", 0), [[0, 64]], ALU.is_ge, -8, 1)
-    sel(R("Z01"), R("ones", 0, 144), [[0, 9], [-1, 16]], ALU.is_ge, 1, 0)
-    for a in (0, 3, 1, 4):
-        sel(R("Ta%d" % a), R("Z01"), [[-16, 9], [-1, 16]], ALU.is_equal, 16 - 2 * a, 1)
-    iota(R("selfb"), [[2, 512]], 0, 0)
+        scl((T.Mbd[:, :, 16 * q:16 * q + 16], "Mbd", 2 * q, 2 * q + 2, 256), (T.matb[:], "matb", 0, 16, 256), R("gm", q, q + 1))
     for b in (0, 1):
-        ts(R("s16n", 512 * b, 512 * b + 512), R("sc", 512 * b, 512 * b + 512), float(G0 - OFF[0]), ALU.add)
+        ts(R("s16n", 512 * b, 512 * b + 512), R("sc", 512 * b, 512 * b + 512), float(G0 - OFF), ALU.add)
         for par in (1, 0):
             mm([(P(6 + par, 256 * b, 256 * b + 256), R("Ip%d" % par, 1 + par - h, 129 + par - h), R("s16n", 512 * b + h, 512 * b + 512, 2)) for h in (0, 1)])
     for par in (1, 0):
-        cp(R("S%d" % par), P(6 + par))
-        ts(R("L%d" % par), R("S%d" % par), float(OFF[0]), ALU.add)
-    ts(R("u0"), R("s16n", 0, 512), float(512 + G0 - OFF[0]), ALU.is_ge, -8192.0, ALU.mult)
+        ts(R("L%d" % par), P(6 + par), float(OFF), ALU.add)
+    ts(R("u0"), R("s16n", 0, 512), float(512 + G0 - OFF), ALU.is_ge, -8192.0, ALU.mult)
     mm([(P(4), I, R("s16n", 0, 512)), (P(4), I, R("u0"))])
-    act(R("hi0"), P(4), AF.Copy)
-    mm([(P(5), R("Ip1", 1, 129), R("s16n", 0, 512)), (P(5), R("Ip1", 1, 129), R("u0")), (P(5), R("Hm"), R("hi0"))])
-    act(R("Snd0"), P(5), AF.Identity, bias=col(11))
-    send_tuples(0)
-    for k in range(4):
-        dma("sp", T.E[k:k + 1, G0:G1], T.fold[0:40, 64 * k:64 * k + 64], [R("fold")], [(None, "rows", k, k + 1)])
-    for k in range(1, 4):
-        dma("sp", T.E[4 * k:4 * k + 4, G0:G1], T.E[0:4, G0:G1], [(None, "rows", 0, 4)], [(None, "rows", 10 + k, 11 + k)])
-    for k in range(1, 8):
-        dma("sp", T.E[16 * k:16 * k + 16, G0:G1], T.E[0:16, G0:G1], [(None, "rows", 0, 20)], [(None, "rows", 20 + k, 21 + k)])
-    done = (None, "rows", 0, 30)
-    dma("sp", T.E[:, G1:WE], T.E[:, G0:GH], [done], [R("E", G1, WE)])
-    dma("sp", T.E[:, G2:G0], T.E[:, G0:GH], [done], [R("E", G2, G0)])
-    dma("sp", T.N1[:, 1024:2560], T.E[:, GH:G1], [done], [R("N1", 1024, 2560)])
-    dma("sp", T.N2[:, 1024:2560], T.E[:, GH:G1], [done], [R("N2", 1024, 2560), R("E", G0, G1)])
-    for out in (R("U", G2, G0), R("W1", G2, G0), R("W2", G0, GH)):
-        copy(out, R("W0", G2, G0))
-    for h in (0, 1):
-        sel(R("Bp%d" % h), R("BP"), [[0, 64], [1, 2]], ALU.is_equal, -h, 0)
-        sel(R("Bn%d" % h), R("BN"), [[0, 64], [1, 2]], ALU.is_equal, -h, 0)
-    for a in (2, 5):
-        sel(R("Ta%d" % a), R("Z01"), [[-16, 9], [-1, 16]], ALU.is_equal, 16 - 2 * a, 1)
-    act(R("nw"), R("nb"), AF.Identity, bias=col(0))
-    act(R("Zbig"), R("Z0"), AF.Copy, scale=BIG)
-    act(R("nXm"), R("Xm"), AF.Copy, scale=-1.0)
-    for k, z in enumerate(("Zpl", "Za", "Zb", "Zt1", "Zt2")):
-        act(R(z), R("Z0"), AF.Copy, scale=col(3 + k))
-    for t in range(3):
-        act(R("self%d" % t), R("selfb"), AF.Identity, bias=col(8 + t))
-        ts(R("ns%d" % t), R("nw"), float(GEN[t]), ALU.add)
+    scl(R("hi0"), P(4), -1.0)
+    mm([(P(5), R("Ip1", 1, 129), x) for x in (R("s16n", 0, 512), R("u0"), R("hi0"))] + [(P(5), R("Ip1", 2, 130), R("hi0"))])
+    shift(R("Snd0"), P(5), col(11))
+    sent = send_tuples(0)
+    bias[0] = 100.0
+    for par in (1, 0):
+        ts(R("S%d" % par), R("L%d" % par), float(-OFF), ALU.add)
+    ts(R("oh"), R("row16"), col(0), ALU.is_equal)
+    ts(col(8), col(1), float(G0 - OFF), ALU.add)
+    ts(col(9), col(1), float(CU - OFF), ALU.add)
+    ts(col(3), col(0), 2.0, ALU.is_lt)
+    ts(col(4), oh(2), float(CU), ALU.mult, col(3), ALU.add)
+    ts(col(5), oh(3), -8192.0, ALU.mult, oh(1), ALU.add)
+    ts(col(12), oh(3), -8192.0, ALU.mult, oh(0), ALU.subtract)
     for t in (1, 2):
-        tt(R("Zs%d" % t), R("Zt%d" % t), R("Ta0"), ALU.add)
+        ts(col(5 + t), oh(2), HIGH - (GH + 512 * t - OFF), ALU.mult, col(12), ALU.add)
+    for h in (0, 1):
+        tt(R("Ch%d" % h), R("Ip1", 2 - h, 130 - h), R("Ip0", 1 - h, 129 - h), ALU.subtract)
+    for k in range(4):
+        ms(R("PR", 64 * k, 64 * k + 64), PRI[k])
+    for k, x in ((13, MID), (14, LIFT - 255.0 / 512), (15, 1.0 / 16)):
+        ms(col(k), x)
+    ms(R("U", PZ, WE), -MID)
+    ms(R("mid"), -MID)
+    ts(R("rewb"), R("rewb"), -MID, ALU.add)
+    ms(R("zero"), 0.0)
+    for name, s in (("Xf", 8191.0), ("Ik", -LIFT), ("Ih", HIGH), ("Is", -16.0), ("Ir", 16 * HIGH - OFF), ("Iw", 16 * BIG), ("In", -1.0)):
+        scl(R(name), I, s)
+    for name, s in (("BP", 8192.0), ("BN", -8192.0), ("RW", col(4))):
+        scl(R(name), Blk, s)
+    tt(R("Xm"), R("Xf"), Blk, ALU.add)
+    scl(R("nXm"), R("Xm"), -1.0)
+    shift(R("nw"), R("nb"), col(0))
+    for t in (0, 1):
+        shift(R("ns%d" % t), R("nb%d" % t), col(0))
+        shift(R("self%d" % t), R("selfb"), col(8 + t))
+    for z, s in (("Zbig", BIG), ("Zpl", col(3)), ("Za", col(4)), ("Zs1", col(6)), ("Zs2", col(7))):
+        scl(R(z), R("Z0"), s)
+    for t in (1, 2):
+        scl(R("Zs%d" % t, 1, 144, 16), R("BlkW", 1, 144, 16), col(5))
 
-    def guests(wname, gen, bank):
-        wrap(P(bank, 0, 64), "Z0", wname, gen)
+    iota(R("fold"), [[0, 4], [1, 64]], 0, 0)
+    iota(R("E", G0, CU), [[64, 40], [0, 64]], 0, 0)
+    copy(R("U", GH, CU), R("mid"))
+    for k, lo, hi, src in ((1, 0, CU, "fold"), (2, 0, GH, "ones"), (2, GH, CU, "zero"), (3, 0, 512, "zero"), (3, 512, CU, "ones")):
+        dma("sp", T.E[k:128:16, lo:hi], T[src][0:(hi - lo) // 32, 0:256], [R(src), R("E", G0, CU)], [(None, "rows", k * CU + lo, k * CU + hi)])
+    dma("sp", T.E[:, CU:PZ], T.E[:, G0:GH], [(None, "rows", 0, 4 * CU)], [R("E")])
+    copy(R("N1", GH, CU), R("E", GH, CU))
+    copy(R("N2", GH, CU), R("E", GH, CU))
+    copy(R("EI"), R("E", G0, GH))
+    sel(R("Z01"), ones(144), [[0, 9], [-1, 16]], ALU.is_ge, 1, 0)
+    for a in (0, 3, 1, 4, 2, 5):
+        sel(R("Ta%d" % a), R("Z01"), [[-16, 9], [-1, 16]], ALU.is_equal, 16 - 2 * a, 1)
+    for h in (0, 1):
+        for out, a in (("Bp", "BP"), ("Bn", "BN"), ("Rw", "RW")):
+            sel(R("%s%d" % (out, h)), R(a), [[0, 64], [1, 2]], ALU.is_equal, -h, 0)
+    old_ghosts(0)
+
+    def guests(bank):
         tt(R("gi"), P(bank, 0, 64), R("nw"), ALU.add)
+        bias[0] += LAZY
         ts(R("gi2"), R("gi"), 511, ALU.bitwise_and)
         cp(R("gl"), R("gi2"))
 
-    def compose(name, t):
-        if t == 2:
-            gat2(name, G1, R(name, 0, G1), "Lb")
-        gat2(name, G0, R(name, GH, WE), "La")
+    def compose(name):
+        gat2(name, G0, R(name, GH, PZ), "La")
 
-    guests("W0", G0, 6)
+    bias[0] = 150.0
+    wrap(P(3, 0, 64), "Z0", "W0", G0)
+    guests(3)
     bias[0] = 0.0
     for t in range(3):
-        W, gen, ev, od = "W%d" % t, GEN[t], t % 2, (t + 1) % 2
-        Lo, Le, So = "L%d" % od, "L%d" % ev, R("S%d" % od)
-        top = G1 if t == 0 else WE
+        W, gen, ev, od = "W%d" % t, CU if t else G0, t % 2, (t + 1) % 2
+        Lo, Le, So = "L%d" % od, "L%d" % ev, "S%d" % od
+        win, top = R(W), WE if t else CU
         obs = [t, 6 + t, 3 + t, 9 + t]
+        K = [P(5, 0, 64), P(7, 0, 64), P(6, 0, 64), P(7, 64, 128)]
 
-        def worth(lname, par, c0, to):
-            rows = gring(R(W, 0, top), lname, c0)
-            for bank in to:
-                mm([(P(bank, 2 * c0 % 512 + r % 2, 2 * c0 % 512 + 128, 2), M(2 * (r // 2) + par), rows[r]) for r in range(16)], (t, bank))
+        def tried(ks, bank):
+            for k in ks:
+                turn(P(bank, 64 * k, 64 * k + 64), obs[k] // 2, "S%d" % (obs[k] % 2), (t, "k", ks[0]))
+            c = (64 * ks[0], 64 * ks[-1] + 64)
+            ts(R("LU", *c), P(bank, *c), float(OFF), ALU.add, float(PZ), ALU.min)
+            if ks[0] in CK:
+                ts(R("ck", *c), R("LU", *c), float(-OFF), ALU.add)
 
+        def codes(bank, c0, c1):
+            return [(bank, R("Ch%d" % h), R("Gg", 2 * c0 + h, 2 * c1, 2)) for h in (0, 1)] + [(bank, R("Ih"), ones(c1 - c0))] * (t > 0)
+
+        bias[0] = URGENT
         if t > 0:
-            for c0 in range(0, 256, 64):
-                rows = gring(R("E"), Lo, c0)
-                mm([(P(5, 2 * c0 + r % 2, 2 * c0 + 128, 2), Z("Zs%d" % t, 2 * (r // 2)), rows[r]) for r in range(16)], (t, "give"))
-            cpa(R("Snd%d" % t), P(5))
-            send_tuples(t)
-        copy(R("U", GH, G1), R(W, GH, G1))
-        for k in range(4):
-            turn(P(4, 64 * k, 64 * k + 64), obs[k] // 2, "S%d" % (obs[k] % 2))
-        tt(R("ckp"), P(4, 0, 256), R("PR"), ALU.add)
-        ts(R("LU", 0, 128), P(4, 0, 128), float(OFF[0]), ALU.add)
-        gat2("Gg", 0, R("Rcv%d" % t), "gl")
-        mm([(P(6), R("Ch%d" % h), R("Gg", h, 1024, 2)) for h in (0, 1)])
-        tt(R("C16"), P(6), R("self%d" % t), ALU.min if t == 1 else ALU.max)
-        ts(R("LB"), R("C16"), float(OFF[t]), ALU.add)
-        for k in (2, 3):
-            turn(P(6, 64 * k - 128, 64 * k - 64), obs[k] // 2, "C16")
-        for k in (0, 1):
-            ts(R("CW", 64 * k, 64 * k + 64), P(6, 64 * k, 64 * k + 64), OFF[t] + PRI[2 + k], ALU.add)
-        tt(R("dif"), R("ckp", 128, 256), R("CW"), ALU.subtract)
-        for b, (pa, pb, n0, n1) in enumerate(YB):
-            c = (n0, n1)
-            own, bank = [P(x, n0 % 512, (n1 - 1) % 512 + 1) for x in (pa, pb)]
-            mm([(own, I, R("rewb", *c))], (t, pa))
-            mm([(bank, I, R("rewb", *c))], (t, pb))
-            for c0 in range(n0 // 2, n1 // 2, 64):
-                worth(Lo, od, c0, [pa])
-                worth(Le, ev, c0, [pa, pb])
-            ts(R("Ai", *c), own, -255.0 / 512, ALU.add, 255.0, ALU.min)
-            for c0 in range(n0 // 2, n1 // 2, 64):
-                worth("LB", od, c0, [pb])
-            tt(R("lt", *c), bank, R("Ai", *c), ALU.is_lt)
-            ts(R("B16", *c), bank, 1024 - 255.0 / 512, ALU.add, 1279.0, ALU.min)
-            for l, r in ((R("Ic"), R("ones", 0, n1 - n0)), (R("BN"), R("lt", *c)), (I, R("B16", *c))):
-                mm([(own, l, r)], (t, "v", b))
-            tt(R("U", gen + n0, gen + n1), own, R("Ai", *c), ALU.max)
-        V = R("U", gen, gen + 1024)
+            for q, c in enumerate(zip(KG, KG[1:])):
+                x = slot(c[1] - c[0])
+                gat(x, R("E", G0, CU), R(Lo, *c), ("dve", "act")[q % 2])
+                fold16(3, 0, c, lambda a: Z("Zs%d" % t, 2 * a), x, (t, "give"))
+            rec("act", lambda e, t=t: g.scalar.activation(T["Snd%d" % t][:, :], T.P3[:, :], AF.Relu), [P(3)], [R("Snd%d" % t)], FIX + 512 * CYC)
+            sent = send_tuples(t)
+            bias[0] = 0.0
+            gat(R(W, G0, GH), R(W, GH, PZ), R("La"), "dve")
+        for q, c in enumerate(zip(GC, GC[1:])):
+            bias[0] = URGENT * (q == 0)
+            bank = P(4 - q, 0, c[1] - c[0])
+            gat(R("Gg", 2 * c[0], 2 * c[1]), R("Rcv%d" % t), R("gl", c[0] // 8, c[1] // 8), "dve")
+            mm(codes(bank, *c))
+            tt(R("C16", *c), bank, R("self%d" % min(t, 1), *c), ALU.min if t else ALU.max)
+            ts(R("LB", *c), R("C16", *c), float(OFF), ALU.add)
+        bias[0] = 0.0
+        if t > 0:
+            copy(R("U", GH, CU), R("mid"), [sent])
+            old_ghosts(t)
+        if t == 2:
+            copy(R("E", CU, PZ), R("EI"), [sent])
+        tried([0, 1], 4)
+        for q, (pa, pb) in enumerate(YP):
+            n = (YB[q], YB[q + 1])
+            w = n[1] - n[0]
+            bias[0] = STEP * (len(YP) - 1 - q)
+            at = {"a": (pa, n[0]), "b": (pb, n[0] - w * (pa == pb)), "e": (pb, n[0])}
+            own, bank = P(pa, 0, w), P(pb, w * (pa == pb), w + w * (pa == pb))
+
+            def worth(lname, par, k, to):
+                for c in units(*n, k):
+                    x = slot(c[1] - c[0])
+                    gat(x, win, R(lname, *c))
+                    for y in to:
+                        fold16(*at[y], c, lambda a: M(2 * a + par), x, (t, at[y][0], y == "e"))
+
+            if q in ONCE:
+                xe, a16, b16 = R("Xe", *n), R("A16", *n), R("B16", *n)
+                mm([(P(pb, 0, w), I, R("rewb", *n))], (t, pb, True))
+                worth(Le, ev, KA[q], "e")
+                shift(xe, P(pb, 0, w), col(14))
+                worth(Lo, od, KA[q], "a")
+                if pa != pb:
+                    tt(a16, own, xe, ALU.add)
+                worth("LB", od, KB[q], "b")
+                if pa == pb:
+                    tt(a16, own, xe, ALU.add)
+                tt(b16, bank, xe, ALU.add)
+                ts(a16, a16, LIFT + 255 - MID, ALU.min)
+                mm([(own, I, a16), (own, R("In"), b16)])
+                either(R("lt", *n), own, AF.Relu, ALU.max, 0.0)
+                mm([(own, I, b16), (own, R("BN"), R("lt", *n))])
+                tt(b16, own, a16, ALU.max)
+                ts(R("U", gen + n[0], gen + n[1]), b16, LIFT + 255 - MID, ALU.min, -LIFT, ALU.add)
+                continue
+            mm([(own, I, R("rewb", *n))], (t, pa, False))
+            mm([(bank, I, R("rewb", *n))], (t, pb, False))
+            for x in ((Lo, od, KA[q], "a"), (Le, ev, KA[q], "ab"))[::-1 if t < 2 else 1]:
+                worth(*x)
+            if pa != pb:
+                ts(R("Ai", *n), own, -255.0 / 512, ALU.add, 255 - MID, ALU.min)
+            worth("LB", od, KB[q], "b")
+            if pa == pb:
+                ts(R("Ai", *n), own, -255.0 / 512, ALU.add, 255 - MID, ALU.min)
+            ts(R("B16", *n), bank, LIFT - 255.0 / 512, ALU.add, LIFT + 255 - MID, ALU.min)
+            tt(R("lt", *n), bank, R("Ai", *n), ALU.is_lt)
+            for l, r in ((R("Ik"), ones(w)), (I, R("B16", *n)), (R("BN"), R("lt", *n))):
+                mm([(own, l, r)], (t, "v", q))
+            tt(R("U", gen + n[0], gen + n[1]), own, R("Ai", *n), ALU.max)
+        Vc = "W%d" % ((t + 1) % 3), CU if t < 2 else G0
+        for n in zip(VC, VC[1:]):
+            a = R("U", gen + n[0], gen + n[1])
+            bias[0] = URGENT if n[0] == 0 else LAZY
+            shift(R(Vc[0], Vc[1] + n[0], Vc[1] + n[1]), a, col(13))
+            bias[0] = 0.0
+            rec("act", lambda e, a=a, n=n: g.scalar.activation(T.Vh[:, n[0]:n[1]], a[0], AF.Identity, bias=col(15)[0]), [a, col(15)], [R("Vh", *n)],
+                FIX + CYC * max(64, a[4]))
         if t < 2:
-            send_ghosts(t + 1, R("U", gen, gen + 512))
-            copy(R("W%d" % (t + 1), GEN[t + 1], GEN[t + 1] + 1024), V)
+            send_ghosts(t + 1, R(Vc[0], CU, CU + 512))
         else:
-            dma("sp", T.yv[:, :], V[0], [V], [])
+            dma("sp", T.yv[:, :], T.W0[:, G0:GH], [R("W0", G0, GH)], [])
         if t > 0:
-            compose("U", t)
-        wrap(P(4, 0, 64), "Zbig", "lt", 0)
-        ts(R("nok"), P(4, 0, 64), 1.0, ALU.min)
-        for k in (0, 1):
-            tt(R("tt1", 64 * k, 64 * k + 64), R("nok"), R("dif", 64 * k, 64 * k + 64), ALU.mult)
-        tt(R("ckp", 128, 256), R("tt1"), R("CW"), ALU.add)
-        for k in (2, 3):
-            ts(R("LU", 64 * k, 64 * k + 64), R("ckp", 64 * k, 64 * k + 64), -PRI[k], ALU.add)
+            compose("U")
+        for q in range(len(MED) - 1):
+            c = (MED[q] // 2, MED[q + 1] // 2)
+            for sgn, b in (("p", 3), ("n", 4)):
+                bank = P(b, 0, c[1] - c[0])
+                mm((codes(bank, *c) if t == 1 else [(bank, I, R("C16", *c))])
+                   + [(bank, R("B%s%d" % (sgn, h)), R("lt", 2 * c[0] + h, 2 * c[1], 2)) for h in (0, 1)])
+            tt(R("u16", *c), P(3, 0, c[1] - c[0]), R(So, *c), ALU.min)
+            tt(R(So, *c), P(4, 0, c[1] - c[0]), R("u16", *c), ALU.max)
+        tried([2, 3], 6)
+        if t != 1:
+            ts(R(Lo), R(So), float(OFF), ALU.add)
+        wrap(P(4, 0, 64), "Z0", "U", gen)
+        ts(R("sv"), P(4, 0, 64), -1.0, ALU.mult)
+        if t < 2:
+            guests(4)
+            bias[0] = 0.0
         for u in range(8):
-            bank, c = P(u % 4), (512 * u, 512 * u + 512)
-            gat(R("Ug", *c), R("U", 0, top), R("LU", 32 * u, 32 * u + 32))
-            mm([(bank, R("nXm"), R("U", gen + 512 * (u % 2), gen + 512 * (u % 2) + 512))], (t, "u", u))
-            mm([(bank, R("Xm"), R("Ug", *c))], (t, "u", u))
-            rec("any", lambda e, o=R("sg", *c)[0], a=bank[0]: g.vector.tensor_scalar(o, a, 0.0, None, ALU.is_gt) if e == "dve"
-                else g.scalar.activation(o, a, AF.Sign), [bank], [R("sg", *c)], FIX + 0.512)
-            if u % 2:
-                k = u // 2
-                wrap(P(4 + k, 0, 64), "Zbig", "sg", 1024 * k)
-                tt(R("uu", 64 * k, 64 * k + 64), P(4 + k, 0, 64), R("ckp", 64 * k, 64 * k + 64), ALU.add)
-                tt(R("mi") if k == 3 else R("m%d" % (k % 2)), R("uu", 64 * k, 64 * k + 64), R("ns%d" % t) if k == 0 else R("m%d" % ((k + 1) % 2)), ALU.max)
+            k, h = divmod(u, 2)
+            b = 2 * (k // 2) + h
+            c, lst = (512 * b, 512 * b + 512), R("LU", 32 * u, 32 * u + 32)
+            if k % 2:
+                least(R("Um", *c), R("U", 0, top), lst, R("Vh", 512 * h, 512 * h + 512))
+            else:
+                gat(R("Ug", *c), R("U", 0, top), lst, "act")
+                mm([(P(b), R("nXm"), R("U", gen + 512 * h, gen + 512 * h + 512))], (t, "u", u))
+                mm([(P(b), R("Xm"), R("Ug", *c))], (t, "u", u))
+                either(R("sg", *c), P(b), AF.Sign, ALU.is_gt, 0.0)
+        for k in (0, 1):
+            mm([(P(4, 64 * k, 64 * k + 64), I, R("sv"))], (t, "m"))
+            wrap(P(4, 64 * k, 64 * k + 64), "Z0", "Um", 1024 * k, (t, "m"))
+        either(R("won"), P(4, 0, 128), AF.Sign, ALU.is_gt, 0.0)
+        for k in range(4):
+            gid = (t, "w", 1 if k % 2 else k)
+            if k // 2 * 2 in CK:
+                mm([(K[k], I, R("ck", 64 * k, 64 * k + 64))], gid)
+            else:
+                turn(K[k], obs[k] // 2, "S%d" % (obs[k] % 2), gid)
+            mm([(K[k], I, R("PR", 64 * k, 64 * k + 64))], gid)
+            if k % 2 == 0:
+                wrap(K[k], "Zbig", "sg", 512 * k, gid)
+        mm([(P(7, 0, 128), R("Iw"), R("won"))], (t, "w", 1))
+        for i, k in enumerate(DO):
+            tt(R("mi") if i == 3 else R("m%d" % (i % 2)), K[k], R("ns%d" % min(t, 1)) if i == 0 else R("m%d" % ((i + 1) % 2)), ALU.max)
         ts(R("mi2"), R("mi"), 8191, ALU.bitwise_and)
         cp(R("Dl"), R("mi2"))
-        for sgn, bank in (("p", 0), ("n", 1)):
-            mm([(P(bank), I, R("C16"))] + [(P(bank), R("Cst"), R("ones"))] * (t == 2)
-               + [(P(bank), R("B%s%d" % (sgn, h)), R("lt", h, 1024, 2)) for h in (0, 1)])
-        tt(R("u32"), P(0), So, ALU.min)
-        tt(So if t < 2 else R("s32"), P(1), R("u32"), ALU.max)
-        ts(R(Lo), So if t < 2 else R("s32"), float(OFF[0]), ALU.add)
         gat2("N1", 0, R("E"), "Dl")
-        if t == 0:
-            ts(R("Dp"), R("mi2"), float(-G0), ALU.add)
-        else:
-            wrap(P(4, 0, 64), "Zpl", "N1", 0)
-            cp(R("Dp"), P(4, 0, 64))
-        gat2("N2", 0, R("N1"), "Dp")
-        wrap(P(5, 0, 64), "Zpl", "N2", 0)
-        cp(R("D2l"), P(5, 0, 64))
-        gat2("E", gen, R("N2"), "D2l")
-        if t < 2:
-            wrap(P(4, 0, 64), "Za" if t == 0 else "Zb", "E", gen)
-            ts(R("La" if t == 0 else "Lb"), P(4, 0, 64), -1024.0 if t == 0 else 1024.0, ALU.add)
-            guests("U", gen, 2)
-            compose("W%d" % (t + 1), t + 1)
         if t > 0:
-            compose("E", t)
+            wrap(P(0, 0, 64), "Zpl", "N1", 0)
+            cp(R("Dp"), P(0, 0, 64))
+        gat2("N2", 0, R("N1"), "Dp" if t else "Dl")
+        if REP:
+            gat2("N1", 0, R("N2"), "Dp" if t else "Dl")
+            gat2("E", gen, R("N1"), "Dp" if t else "Dl")
+        else:
+            wrap(P(1, 0, 64), "Zpl", "N2", 0)
+            cp(R("D2l"), P(1, 0, 64))
+            gat2("E", gen, R("N2"), "D2l")
+        if t > 0:
+            compose("E")
+        if t < 2:
+            wrap(P(0, 0, 64), "Za", "E", G0)
+            ts(R("La"), P(0, 0, 64), float(-GH), ALU.add)
+        if t == 1:
+            mm([(P(4), R("Ir"), ones(512)), (P(4), R("Is"), R(So))] + [(P(4), R("Rw%d" % h), R("E", CU + h, PZ, 2)) for h in (0, 1)])
+            tt(R(So), P(4), R(So), ALU.min)
+            ts(R(Lo), R(So), float(OFF), ALU.add)
 
     for q in range(len(FIN) - 1):
         n0, n1 = FIN[q], FIN[q + 1]
         for par in (0, 1):
-            for c0 in range(n0 // 2, n1 // 2, 64):
-                rows = gring(R("E"), "L%d" % par, c0)
-                mm([(P(q, 2 * c0 - n0 + r % 2, 2 * c0 + 128 - n0, 2), Z("Zpl", 2 * (r // 2) + par), rows[r]) for r in range(16)], ("end", q))
-        cpa(R("outf", n0, n1), P(q, 0, n1 - n0))
+            for c in units(n0, n1, KF[q]):
+                x = slot(c[1] - c[0])
+                gat(x, R("E"), R("L%d" % par, *c))
+                fold16(q, n0, c, lambda a: Z("Zpl", 2 * a + par), x, ("end", q))
+        scl(R("outf", n0, n1), P(q, 0, n1 - n0), 1.0)
         dma("sp", T.ys[:, n0:n1], T.outf[:, n0:n1], [R("outf", n0, n1)], [])
 
     n = len(ops)
@@ -462,13 +597,14 @@ def rank_program(g, core, T, topo):
     while ready:
         t0, e = min((max(free.get(x, 0.0), est[i]), x) for i in ready for x in (("act", "dve") if ops[i]["eng"] == "any" else (ops[i]["eng"],)))
         mine_e = [i for i in ready if ops[i]["eng"] == e or (ops[i]["eng"] == "any" and e in ("act", "dve"))]
-        i = max((i for i in mine_e if est[i] <= t0), key=lambda i: rest[i] + (OWN if ops[i]["eng"] == e else 0))
-        soon = [j for j in mine_e if rest[j] > rest[i] and ops[j]["eng"] == e and est[j] - t0 < PATIENCE * ops[i]["cost"]]
+        key = {i: rest[i] + (OWN + QUICK * (ops[i]["cost"] < SHORT) if ops[i]["eng"] == e == "dve" else 0) for i in mine_e}
+        i = max((i for i in mine_e if est[i] <= t0), key=key.get)
+        soon = [j for j in mine_e if key[j] > key[i] and (ops[j]["eng"] == e or ops[j]["cost"] < SHORT) and est[j] - t0 < PATIENCE * ops[i]["cost"]]
         if soon:
-            i = max(soon, key=lambda j: rest[j])
+            i = max(soon, key=key.get)
         o = ops[i]
         o["eng"] = e
-        free[e] = max(t0, est[i]) + o["cost"]
+        free[e] = max(t0, est[i]) + o["fast" if e == "dve" else "cost"]
         end[i] = free[e] + o["lat"]
         ready.remove(i)
         line.append(i)
@@ -511,7 +647,7 @@ def rank_program(g, core, T, topo):
                 count[e] = count.get(e, 0) + 1
                 o["sem"], o["cnt"] = "c_" + e, count[e]
                 ins.then_inc(T.sem[o["sem"]], 1)
-            elif o["sem"] is not None and e != "pool":
+            elif o["sem"] is not None and o["sem"][0] == "d":
                 ins.then_inc(T.sem[o["sem"]], 16)
         if o["sem"] is not None:
             final[o["sem"]] = max(final.get(o["sem"], 0), o["cnt"])

from concourse.bass import DstId, RemoteDMATransfer
from concourse.mybir import AluOpType as ALU, ActivationFunctionType as AF

G0, GH, CU, PZ, WE = 0, 1024, 2560, 3584, 3600
OFF = 1792
HIGH = 2048.0
LIFT = 1280.0
BIG = 65536.0
MID = 128.0
PRI = [8192.0 * (4 - k) + OFF for k in (0, 2, 1, 3)]
RING = 24576
YB = [0, 512, 896, 1024]
YP = [(0, 1), (2, 5), (6, 7)]
KA = [128, 96, 64]
KB = [64, 64, 64]
KG = [0, 64, 128, 176, 256]
GC = [0, 256, 512]
VC = [0, 512, 896, 1024]
MED = [0, 512, 1024]
FIN = [0, 512, 896, 1024]
KF = [128, 64, 64]
DO = [0, 1, 3, 2]
CYC = 0.83e-3
GATHER = 1.3e-3
PE = 0.43e-3
FIX = 0.06
HOP = 0.14
ONCE = [0]
REP = 1
CK = [0, 2]
RELAY = []
FARG = [6.0, 7.0, 7.0]
FART = [8.0, 5.0, 7.0]
PATIENCE = 0.1
OWN = 8.0
QUICK = 6.0
SHORT = 0.7
URGENT = 20.0
LAZY = -8.0
STEP = 0.2

SCRATCH = {}
def _sb(names, n, d):
    for x in names.split():
        SCRATCH[x] = ("sbuf", [128, n], d)
_sb("W1 W2 E", PZ, "bfloat16")
_sb("U", WE, "bfloat16")
_sb("W0 N1 N2", CU, "bfloat16")
_sb("rewb lt Gg EI", 1024, "bfloat16")
_sb("GR", RING, "bfloat16")
_sb("Ug sg", 2048, "bfloat16")
_sb("Um", 2048, "float16")
_sb("mid", 1536, "bfloat16")
_sb("Rcv0 Rcv1 Rcv2 Snd0 Snd1 Snd2 ones hi0 u0", 512, "bfloat16")
_sb("BlkA BlkW Z0 Z01 Zbig Zpl Za Zs1 Zs2 Ta0 Ta1 Ta2 Ta3 Ta4 Ta5", 144, "bfloat16")
_sb("Ib Ip0 Ip1", 130, "bfloat16")
_sb("Ch0 Ch1 BP BN RW Bp0 Bp1 Bn0 Bn1 Rw0 Rw1 Xm nXm Ik Ih Is Ir Iw In won", 128, "bfloat16")
_sb("fold zero PR", 256, "bfloat16")
_sb("sc Ai", 1024, "int32")
_sb("s16n A16 B16", 1024, "float16")
_sb("ck", 256, "float16")
_sb("S0 S1 C16 u16", 512, "float16")
_sb("sv", 64, "float16")
_sb("L0 L1 LB", 512, "uint16")
_sb("LU", 256, "uint16")
_sb("gl Dl Dp D2l La", 64, "uint16")
_sb("self0 self1 selfb", 512, "float32")
_sb("outf Vh Xe", 1024, "float32")
_sb("Xf", 128, "float32")
_sb("nw nb nb0 nb1 ns0 ns1 m0 m1", 64, "float32")
_sb("gi gi2 mi mi2", 64, "int32")
_sb("row16 oh cols gm", 16, "float32")
_sb("pi", 4, "int32")
SCRATCH["matb"] = ("sbuf", [128, 16, 16], "bfloat16")
SCRATCH["Mbd"] = ("sbuf", [128, 16, 128], "bfloat16")
for _b in range(8):
    SCRATCH["P%d" % _b] = ("psum", [128, 512], "float32")

SEMAPHORES = ["c_pe", "c_dve", "c_act", "c_pool"] + [x + str(t) for x in ("sn", "gp") for t in range(3)] + ["gh%d" % t for t in range(3)] + ["tp%d" % t for t in range(3)] \
    + ["sg%d" % t for t in range(3)] + ["st%d" % t for t in range(3)] + ["d%d" % i for i in range(48)]


def rank_program(g, core, T, topo):
    rank = T.rank_of(core)
    if rank is None:
        return
    NR = len(T.cores)
    Q = {"pool": g, "pe": g.tensor, "dve": g.vector, "act": g.scalar, "sp": g.sync}
    ops, hist, banks, prev, nd, ring, bias = [], {}, {}, {}, [0], [0], [0.0]

    def R(name, lo=0, hi=None, step=1):
        if hi is None:
            hi = SCRATCH[name][1][1]
        ap = T[name][:, lo:hi:step] if step > 1 else T[name][:, lo:hi]
        return (ap, name, lo, hi, (hi - lo + step - 1) // step)

    def rec(eng, fn, reads, writes, cost, lat=0.0, sem=None, cnt=0, gid=None, after=(), fast=None):
        i, deps = len(ops), set(after)
        for rs, wr in ((reads, False), (writes, True)):
            for r in rs:
                name, lo, hi = r[1:4]
                if name[0] == "P" and name[1:].isdigit():
                    b = banks.setdefault(name, [[], []])
                    deps.update(j for j in b[0] if j < i)
                    if eng == "pe":
                        deps.update(j for j in b[1] if j < i and (gid is None or ops[j]["gid"] != gid))
                        b[1].append(i)
                    else:
                        deps.update(b[1])
                        b[0], b[1] = [i], []
                    continue
                h = hist.setdefault(name, [])
                deps.update(j for (l2, h2, j, w2) in h if j < i and l2 < hi and lo < h2 and (wr or w2))
                if wr:
                    h[:] = [e for e in h if not (lo <= e[0] and e[1] <= hi)]
                h.append((lo, hi, i, wr))
        order = [prev[eng]] if eng in prev else []
        if eng in ("pool", "sp"):
            prev[eng] = i
        ops.append({"eng": eng, "fn": fn, "deps": deps, "order": order, "cost": cost, "lat": lat, "sem": sem, "cnt": cnt, "gid": gid, "bias": bias[0],
                    "fast": fast or cost})
        return i

    def num(x):
        return x[0] if isinstance(x, tuple) else x

    def aps(*xs):
        return [x for x in xs if isinstance(x, tuple)]

    def dur(out, a, rate=None):
        if rate is None:
            rate = 0.5 if all(SCRATCH[x[1]][2].endswith("16") for x in (out, a)) else 1
        return FIX + max(64, rate * out[4]) * CYC

    def ts(out, a, s1, op0, s2=None, op1=None):
        if op1 is None:
            rec("dve", lambda e: g.vector.tensor_scalar(out[0], a[0], num(s1), None, op0), aps(a, s1), [out], dur(out, a))
        else:
            rec("dve", lambda e: g.vector.tensor_scalar(out[0], a[0], num(s1), num(s2), op0, op1), aps(a, s1, s2), [out], dur(out, a))

    def tt(out, a, b, op):
        rec("dve", lambda e: g.vector.tensor_tensor(out[0], a[0], b[0], op), [a, b], [out], dur(out, a, 1 if SCRATCH[a[1]][0] == "psum" else 2))

    def cp(out, a):
        rec("dve", lambda e: g.vector.tensor_copy(out[0], a[0]), [a], [out], dur(out, a))

    def ms(out, c):
        rec("dve", lambda e: g.vector.memset(out[0], c), [], [out], dur(out, out))

    def either(out, a, func, op, s):
        def fn(e):
            if e == "dve":
                return g.vector.tensor_scalar(out[0], a[0], num(s), None, op)
            if op == ALU.add:
                return g.scalar.activation(out[0], a[0], func, bias=num(s))
            return g.scalar.activation(out[0], a[0], func, scale=num(s) if op == ALU.mult else 1.0)
        rec("any", fn, aps(a, s), [out], dur(out, a, 1), fast=dur(out, a))

    def scl(out, a, s):
        either(out, a, AF.Copy, ALU.mult, s)

    def shift(out, a, s):
        either(out, a, AF.Identity, ALU.add, s)

    def mm(calls, gid=None):
        def fn(flags):
            for k, (o, l, r) in enumerate(calls):
                ins = g.tensor.matmul(o[0], l[0], r[0], flags[0] and k == 0, flags[1] and k == len(calls) - 1)
            return ins
        rec("pe", fn, [x for c in calls for x in c[1:]], [calls[0][0]], sum(max(64, c[2][4]) for c in calls) * PE, gid=gid)

    def iota(out, pattern, base, cm):
        if SCRATCH[out[1]][2] == "int32":
            rec("pool", lambda e: g.iota(out[0], pattern, base, cm), [], [out], 0.13 + 2 * CYC * out[4])
        else:
            rec("pool", lambda e: g.iota(out[0], pattern, base, cm, allow_small_or_imprecise_dtypes=True), [], [out], 0.13 + 2 * CYC * out[4])

    def sel(out, a, pattern, op, base, cm):
        rec("pool", lambda e: g.affine_select(out[0], a[0], pattern, op, 0.0, base, cm), [a], [out], 0.17 + 2 * CYC * out[4])

    def dma(eng, out, in_, reads, writes, lat=2.5, after=()):
        nd[0] += 1
        rec(eng, lambda e: g.dma_start(out, in_, accum_op=ALU.add) if eng == "pool" else Q[eng].dma_start(out, in_), reads, writes, 0.1, lat,
            "d%d" % (nd[0] - 1), 16, after=after)

    def old_ghosts(t):
        u = R("U", GH, CU)
        dma("pool", u[0], T["W%d" % t][:, GH:CU], [R("W%d" % t, GH, CU), u], [u], 4.0)

    def copy(out, a, after=()):
        dma("sp", out[0], a[0], [a], [out], 3.0, after)

    def gat(out, win, off, eng="any"):
        rec(eng, lambda e: g.vector.tensor_copy(out[0], win[0].indirect(off[0])) if e == "dve"
            else g.scalar.activation(out[0], win[0].indirect(off[0]), AF.Copy), [win, off], [out], FIX + GATHER * out[4])

    def least(out, win, off, old):
        rec("dve", lambda e: g.vector.tensor_tensor(out[0], win[0].indirect(off[0]), old[0], ALU.min), [win, off, old], [out], FIX + GATHER * out[4])

    def gat2(oname, o0, win, lname):
        for hf in (0, 1):
            gat(R(oname, o0 + 512 * hf, o0 + 512 * hf + 512), win, R(lname, 32 * hf, 32 * hf + 32))

    def slot(k):
        if ring[0] + 16 * k > RING:
            ring[0] = 0
        ring[0] += 16 * k
        return R("GR", ring[0] - 16 * k, ring[0])

    def rows(x):
        return [R(x[1], x[2] + r, x[3], 16) for r in range(16)]

    def units(n0, n1, k):
        return [(c0, min(c0 + k, n1 // 2)) for c0 in range(n0 // 2, n1 // 2, k)]

    def fold16(bank, base, c, mats, x, gid):
        mm([(P(bank, 2 * c[0] - base + r % 2, 2 * c[1] - base, 2), mats(r // 2), v) for r, v in enumerate(rows(x))], gid)

    def Z(name, j):
        return R(name, 16 - j, 144 - j)

    def wrap(out, zname, src, lo, gid=None):
        mm([(out, Z(zname, j), R(src, lo + j, lo + 1024, 16)) for j in range(16)], gid)

    def turn(out, a, src, gid=None):
        mm([(out, Z("Ta%d" % a, 2 * j), R(src, j, 512, 8)) for j in range(8)], gid)

    def M(o, name="Mbd"):
        return (T[name][:, o, :], name, 0, 16, 128)

    def col(k):
        return R("cols", k, k + 1)

    def oh(k):
        return R("oh", k, k + 1)

    def P(b, lo=0, hi=512, step=1):
        return R("P%d" % b, lo, hi, step)

    def ones(n):
        return R("ones", 0, n)

    def plan(src):
        others = [c for c in T.cores if c != src]
        far = [c for c in others if topo.chip(c) != topo.chip(src)]
        out, used = {}, []
        for i, c in enumerate(far):
            e = topo.engines(src, c)
            k = len(e) // len(far)
            out[c] = e[i * k:(i + 1) * k]
            used += e
        for c in others:
            if c not in out:
                out[c] = [e for e in topo.engines(src, c) if e not in used][::2]
        return out, sorted(set(used))

    def bits(es):
        return sum(1 << e for e in es)

    def dst(c):
        a = topo.addr(c)
        return DstId(rid=a[0], pnc=a[1])

    mine, wide = plan(core)
    near = [c for c in mine if topo.chip(c) == topo.chip(core)][0]
    twin = [c for c in mine if c != near and topo.die(c) == topo.die(core)][0]

    def send_ghosts(t, src):
        W = "W%d" % t

        def place(of, at):
            d = (T.rank_of(of) - T.rank_of(at)) % NR
            return R(W, GH + 512 * (d - 1), GH + 512 * d)

        def write(a, of, part, lsem, lat):
            trs = [RemoteDMATransfer(dst_ids=[dst(c)], dma_engine_mask=bits(es), remote_sem=T.sem[sem], src=a[0], dst=place(of, c)[0]) for c, es, sem in part]
            return rec("pool", lambda e: g.remote_dma_fused(trs, local_sem=T.sem[lsem]), [a], [], 0.7, lat, lsem, sum(len(es) for c, es, sem in part))

        if t in RELAY:
            i = write(src, core, [(twin, wide, "gp%d" % t), (near, mine[near], "gh%d" % t)], "sg%d" % t, FARG[t])
            rec("ext", None, [], [place(twin, core)], 0.0, 0.0, "gp%d" % t, len(wide), after=[i])
            j = write(place(twin, core), twin, [(near, mine[near], "gh%d" % t)], "sn%d" % t, 4.0)
            rec("ext", None, [], [place(c, core) for c in mine if c != twin], 0.0, 0.0, "gh%d" % t, 2 * len(mine[near]), after=[j])
        else:
            i = write(src, core, [(c, mine[c], "gh%d" % t) for c in mine], "sg%d" % t, FARG[t])
            rec("ext", None, [], [R(W, GH, CU)], 0.0, 0.0, "gh%d" % t, sum(len(plan(c)[0][core]) for c in mine), after=[i])
        return i

    def send_tuples(t):
        c = T.cores[(rank - t - 1) % NR]
        tr = RemoteDMATransfer(dst_ids=[dst(c)], dma_engine_mask=bits(wide), remote_sem=T.sem["tp%d" % t], src=T["Snd%d" % t][:, :], dst=T["Rcv%d" % t][:, :])
        i = rec("pool", lambda e: g.remote_dma_fused([tr], local_sem=T.sem["st%d" % t]), [R("Snd%d" % t)], [], 1.0, FART[t], "st%d" % t, len(wide))
        rec("ext", None, [], [R("Rcv%d" % t)], 0.0, 0.0, "tp%d" % t, len(plan(T.cores[(rank + t + 1) % NR])[1]), after=[i])
        return i

    bias[0] = 200.0
    dma("sp", T.W0[:, G0:G0 + 512], T.v0[:, 0:512], [], [R("W0", G0, G0 + 512)], 2.2)
    dma("act", T.sc[:, 0:512], T.succ[:, 0:512], [], [R("sc", 0, 512)], 3.0)
    dma("sp", T.matb[:], T.mat[:, :], [], [R("matb")], 3.2)
    dma("act", T.sc[:, 512:1024], T.succ[:, 512:1024], [], [R("sc", 512, 1024)], 4.2)
    dma("sp", T.W0[:, G0 + 512:GH], T.v0[:, 512:1024], [], [R("W0", G0 + 512, GH)], 4.5)
    dma("sp", T.rewb[:, :], T.rew[:, :], [], [R("rewb")], 5.5)

    ms(ones(512), 1.0)
    iota(R("pi", 0, 1), [[0, 1]], 0, 1)
    iota(R("row16"), [[1, 16]], 0, 0)
    sel(R("Ib"), ones(130), [[-1, 130]], ALU.is_equal, 1, 1)
    sel(R("BlkA"), ones(144), [[-16, 9], [0, 16]], ALU.is_ge, 16, 1)
    sel(R("BlkW"), R("BlkA"), [[16, 9], [0, 16]], ALU.is_ge, -1, -1)
    send_ghosts(0, R("W0", G0, G0 + 512))
    sel(R("Z0"), R("BlkW"), [[0, 9], [1, 16]], ALU.is_equal, 0, 0)
    iota(R("nb"), [[16, 64]], int(16 * MID), 0)
    iota(R("selfb"), [[2, 512]], 0, 0)
    iota(R("nb0"), [[16, 64]], int(16 * BIG) + G0, 0)
    iota(R("nb1"), [[16, 64]], int(16 * BIG) + CU, 0)
    I, Blk = R("Ib", 1, 129), R("BlkW", 16, 144)
    ts(R("pi", 1, 2), R("pi", 0, 1), 15, ALU.bitwise_and)
    ts(R("pi", 2, 3), R("pi", 0, 1), 1, ALU.bitwise_and)
    cp(R("cols", 0, 2), R("pi", 1, 3))
    ts(col(2), col(1), -1.0, ALU.mult, 1.0, ALU.add)
    scl(R("Ip1"), R("Ib"), col(1))
    scl(R("Ip0"), R("Ib"), col(2))
    scl(col(11), col(2), -1024.0)
    scl(R("gm", 0, 8), R("BlkW", 16, 144, 16), 1.0 / 256)
    for q in range(8):
        scl((T.Mbd[:, :, 16 * q:16 * q + 16], "Mbd", 2 * q, 2 * q + 2, 256), (T.matb[:], "matb", 0, 16, 256), R("gm", q, q + 1))
    for b in (0, 1):
        ts(R("s16n", 512 * b, 512 * b + 512), R("sc", 512 * b, 512 * b + 512), float(G0 - OFF), ALU.add)
        for par in (1, 0):
            mm([(P(6 + par, 256 * b, 256 * b + 256), R("Ip%d" % par, 1 + par - h, 129 + par - h), R("s16n", 512 * b + h, 512 * b + 512, 2)) for h in (0, 1)])
    for par in (1, 0):
        ts(R("L%d" % par), P(6 + par), float(OFF), ALU.add)
    ts(R("u0"), R("s16n", 0, 512), float(512 + G0 - OFF), ALU.is_ge, -8192.0, ALU.mult)
    mm([(P(4), I, R("s16n", 0, 512)), (P(4), I, R("u0"))])
    scl(R("hi0"), P(4), -1.0)
    mm([(P(5), R("Ip1", 1, 129), x) for x in (R("s16n", 0, 512), R("u0"), R("hi0"))] + [(P(5), R("Ip1", 2, 130), R("hi0"))])
    shift(R("Snd0"), P(5), col(11))
    sent = send_tuples(0)
    bias[0] = 100.0
    for par in (1, 0):
        ts(R("S%d" % par), R("L%d" % par), float(-OFF), ALU.add)
    ts(R("oh"), R("row16"), col(0), ALU.is_equal)
    ts(col(8), col(1), float(G0 - OFF), ALU.add)
    ts(col(9), col(1), float(CU - OFF), ALU.add)
    ts(col(3), col(0), 2.0, ALU.is_lt)
    ts(col(4), oh(2), float(CU), ALU.mult, col(3), ALU.add)
    ts(col(5), oh(3), -8192.0, ALU.mult, oh(1), ALU.add)
    ts(col(12), oh(3), -8192.0, ALU.mult, oh(0), ALU.subtract)
    for t in (1, 2):
        ts(col(5 + t), oh(2), HIGH - (GH + 512 * t - OFF), ALU.mult, col(12), ALU.add)
    for h in (0, 1):
        tt(R("Ch%d" % h), R("Ip1", 2 - h, 130 - h), R("Ip0", 1 - h, 129 - h), ALU.subtract)
    for k in range(4):
        ms(R("PR", 64 * k, 64 * k + 64), PRI[k])
    for k, x in ((13, MID), (14, LIFT - 255.0 / 512), (15, 1.0 / 16)):
        ms(col(k), x)
    ms(R("U", PZ, WE), -MID)
    ms(R("mid"), -MID)
    ts(R("rewb"), R("rewb"), -MID, ALU.add)
    ms(R("zero"), 0.0)
    for name, s in (("Xf", 8191.0), ("Ik", -LIFT), ("Ih", HIGH), ("Is", -16.0), ("Ir", 16 * HIGH - OFF), ("Iw", 16 * BIG), ("In", -1.0)):
        scl(R(name), I, s)
    for name, s in (("BP", 8192.0), ("BN", -8192.0), ("RW", col(4))):
        scl(R(name), Blk, s)
    tt(R("Xm"), R("Xf"), Blk, ALU.add)
    scl(R("nXm"), R("Xm"), -1.0)
    shift(R("nw"), R("nb"), col(0))
    for t in (0, 1):
        shift(R("ns%d" % t), R("nb%d" % t), col(0))
        shift(R("self%d" % t), R("selfb"), col(8 + t))
    for z, s in (("Zbig", BIG), ("Zpl", col(3)), ("Za", col(4)), ("Zs1", col(6)), ("Zs2", col(7))):
        scl(R(z), R("Z0"), s)
    for t in (1, 2):
        scl(R("Zs%d" % t, 1, 144, 16), R("BlkW", 1, 144, 16), col(5))

    iota(R("fold"), [[0, 4], [1, 64]], 0, 0)
    iota(R("E", G0, CU), [[64, 40], [0, 64]], 0, 0)
    copy(R("U", GH, CU), R("mid"))
    for k, lo, hi, src in ((1, 0, CU, "fold"), (2, 0, GH, "ones"), (2, GH, CU, "zero"), (3, 0, 512, "zero"), (3, 512, CU, "ones")):
        dma("sp", T.E[k:128:16, lo:hi], T[src][0:(hi - lo) // 32, 0:256], [R(src), R("E", G0, CU)], [(None, "rows", k * CU + lo, k * CU + hi)])
    dma("sp", T.E[:, CU:PZ], T.E[:, G0:GH], [(None, "rows", 0, 4 * CU)], [R("E")])
    copy(R("N1", GH, CU), R("E", GH, CU))
    copy(R("N2", GH, CU), R("E", GH, CU))
    copy(R("EI"), R("E", G0, GH))
    sel(R("Z01"), ones(144), [[0, 9], [-1, 16]], ALU.is_ge, 1, 0)
    for a in (0, 3, 1, 4, 2, 5):
        sel(R("Ta%d" % a), R("Z01"), [[-16, 9], [-1, 16]], ALU.is_equal, 16 - 2 * a, 1)
    for h in (0, 1):
        for out, a in (("Bp", "BP"), ("Bn", "BN"), ("Rw", "RW")):
            sel(R("%s%d" % (out, h)), R(a), [[0, 64], [1, 2]], ALU.is_equal, -h, 0)
    old_ghosts(0)

    def guests(bank):
        tt(R("gi"), P(bank, 0, 64), R("nw"), ALU.add)
        bias[0] += LAZY
        ts(R("gi2"), R("gi"), 511, ALU.bitwise_and)
        cp(R("gl"), R("gi2"))

    def compose(name):
        gat2(name, G0, R(name, GH, PZ), "La")

    bias[0] = 150.0
    wrap(P(3, 0, 64), "Z0", "W0", G0)
    guests(3)
    bias[0] = 0.0
    for t in range(3):
        W, gen, ev, od = "W%d" % t, CU if t else G0, t % 2, (t + 1) % 2
        Lo, Le, So = "L%d" % od, "L%d" % ev, "S%d" % od
        win, top = R(W), WE if t else CU
        obs = [t, 6 + t, 3 + t, 9 + t]
        K = [P(5, 0, 64), P(7, 0, 64), P(6, 0, 64), P(7, 64, 128)]

        def tried(ks, bank):
            for k in ks:
                turn(P(bank, 64 * k, 64 * k + 64), obs[k] // 2, "S%d" % (obs[k] % 2), (t, "k", ks[0]))
            c = (64 * ks[0], 64 * ks[-1] + 64)
            ts(R("LU", *c), P(bank, *c), float(OFF), ALU.add, float(PZ), ALU.min)
            if ks[0] in CK:
                ts(R("ck", *c), R("LU", *c), float(-OFF), ALU.add)

        def codes(bank, c0, c1):
            return [(bank, R("Ch%d" % h), R("Gg", 2 * c0 + h, 2 * c1, 2)) for h in (0, 1)] + [(bank, R("Ih"), ones(c1 - c0))] * (t > 0)

        bias[0] = URGENT
        if t > 0:
            for q, c in enumerate(zip(KG, KG[1:])):
                x = slot(c[1] - c[0])
                gat(x, R("E", G0, CU), R(Lo, *c), ("dve", "act")[q % 2])
                fold16(3, 0, c, lambda a: Z("Zs%d" % t, 2 * a), x, (t, "give"))
            rec("act", lambda e, t=t: g.scalar.activation(T["Snd%d" % t][:, :], T.P3[:, :], AF.Relu), [P(3)], [R("Snd%d" % t)], FIX + 512 * CYC)
            sent = send_tuples(t)
            bias[0] = 0.0
            gat(R(W, G0, GH), R(W, GH, PZ), R("La"), "dve")
        for q, c in enumerate(zip(GC, GC[1:])):
            bias[0] = URGENT * (q == 0)
            bank = P(4 - q, 0, c[1] - c[0])
            gat(R("Gg", 2 * c[0], 2 * c[1]), R("Rcv%d" % t), R("gl", c[0] // 8, c[1] // 8), "dve")
            mm(codes(bank, *c))
            tt(R("C16", *c), bank, R("self%d" % min(t, 1), *c), ALU.min if t else ALU.max)
            ts(R("LB", *c), R("C16", *c), float(OFF), ALU.add)
        bias[0] = 0.0
        if t > 0:
            copy(R("U", GH, CU), R("mid"), [sent])
            old_ghosts(t)
        if t == 2:
            copy(R("E", CU, PZ), R("EI"), [sent])
        tried([0, 1], 4)
        for q, (pa, pb) in enumerate(YP):
            n = (YB[q], YB[q + 1])
            w = n[1] - n[0]
            bias[0] = STEP * (len(YP) - 1 - q)
            at = {"a": (pa, n[0]), "b": (pb, n[0] - w * (pa == pb)), "e": (pb, n[0])}
            own, bank = P(pa, 0, w), P(pb, w * (pa == pb), w + w * (pa == pb))

            def worth(lname, par, k, to):
                for c in units(*n, k):
                    x = slot(c[1] - c[0])
                    gat(x, win, R(lname, *c))
                    for y in to:
                        fold16(*at[y], c, lambda a: M(2 * a + par), x, (t, at[y][0], y == "e"))

            if q in ONCE:
                xe, a16, b16 = R("Xe", *n), R("A16", *n), R("B16", *n)
                mm([(P(pb, 0, w), I, R("rewb", *n))], (t, pb, True))
                worth(Le, ev, KA[q], "e")
                shift(xe, P(pb, 0, w), col(14))
                worth(Lo, od, KA[q], "a")
                if pa != pb:
                    tt(a16, own, xe, ALU.add)
                worth("LB", od, KB[q], "b")
                if pa == pb:
                    tt(a16, own, xe, ALU.add)
                tt(b16, bank, xe, ALU.add)
                ts(a16, a16, LIFT + 255 - MID, ALU.min)
                mm([(own, I, a16), (own, R("In"), b16)])
                either(R("lt", *n), own, AF.Relu, ALU.max, 0.0)
                mm([(own, I, b16), (own, R("BN"), R("lt", *n))])
                tt(b16, own, a16, ALU.max)
                ts(R("U", gen + n[0], gen + n[1]), b16, LIFT + 255 - MID, ALU.min, -LIFT, ALU.add)
                continue
            mm([(own, I, R("rewb", *n))], (t, pa, False))
            mm([(bank, I, R("rewb", *n))], (t, pb, False))
            for x in ((Lo, od, KA[q], "a"), (Le, ev, KA[q], "ab"))[::-1 if t < 2 else 1]:
                worth(*x)
            if pa != pb:
                ts(R("Ai", *n), own, -255.0 / 512, ALU.add, 255 - MID, ALU.min)
            worth("LB", od, KB[q], "b")
            if pa == pb:
                ts(R("Ai", *n), own, -255.0 / 512, ALU.add, 255 - MID, ALU.min)
            ts(R("B16", *n), bank, LIFT - 255.0 / 512, ALU.add, LIFT + 255 - MID, ALU.min)
            tt(R("lt", *n), bank, R("Ai", *n), ALU.is_lt)
            for l, r in ((R("Ik"), ones(w)), (I, R("B16", *n)), (R("BN"), R("lt", *n))):
                mm([(own, l, r)], (t, "v", q))
            tt(R("U", gen + n[0], gen + n[1]), own, R("Ai", *n), ALU.max)
        Vc = "W%d" % ((t + 1) % 3), CU if t < 2 else G0
        for n in zip(VC, VC[1:]):
            a = R("U", gen + n[0], gen + n[1])
            bias[0] = URGENT if n[0] == 0 else LAZY
            shift(R(Vc[0], Vc[1] + n[0], Vc[1] + n[1]), a, col(13))
            bias[0] = 0.0
            rec("act", lambda e, a=a, n=n: g.scalar.activation(T.Vh[:, n[0]:n[1]], a[0], AF.Identity, bias=col(15)[0]), [a, col(15)], [R("Vh", *n)],
                FIX + CYC * max(64, a[4]))
        if t < 2:
            send_ghosts(t + 1, R(Vc[0], CU, CU + 512))
        else:
            dma("sp", T.yv[:, :], T.W0[:, G0:GH], [R("W0", G0, GH)], [])
        if t > 0:
            compose("U")
        for q in range(len(MED) - 1):
            c = (MED[q] // 2, MED[q + 1] // 2)
            for sgn, b in (("p", 3), ("n", 4)):
                bank = P(b, 0, c[1] - c[0])
                mm((codes(bank, *c) if t == 1 else [(bank, I, R("C16", *c))])
                   + [(bank, R("B%s%d" % (sgn, h)), R("lt", 2 * c[0] + h, 2 * c[1], 2)) for h in (0, 1)])
            tt(R("u16", *c), P(3, 0, c[1] - c[0]), R(So, *c), ALU.min)
            tt(R(So, *c), P(4, 0, c[1] - c[0]), R("u16", *c), ALU.max)
        tried([2, 3], 6)
        if t != 1:
            ts(R(Lo), R(So), float(OFF), ALU.add)
        wrap(P(4, 0, 64), "Z0", "U", gen)
        ts(R("sv"), P(4, 0, 64), -1.0, ALU.mult)
        if t < 2:
            guests(4)
            bias[0] = 0.0
        for u in range(8):
            k, h = divmod(u, 2)
            b = 2 * (k // 2) + h
            c, lst = (512 * b, 512 * b + 512), R("LU", 32 * u, 32 * u + 32)
            if k % 2:
                least(R("Um", *c), R("U", 0, top), lst, R("Vh", 512 * h, 512 * h + 512))
            else:
                gat(R("Ug", *c), R("U", 0, top), lst, "act")
                mm([(P(b), R("nXm"), R("U", gen + 512 * h, gen + 512 * h + 512))], (t, "u", u))
                mm([(P(b), R("Xm"), R("Ug", *c))], (t, "u", u))
                either(R("sg", *c), P(b), AF.Sign, ALU.is_gt, 0.0)
        for k in (0, 1):
            mm([(P(4, 64 * k, 64 * k + 64), I, R("sv"))], (t, "m"))
            wrap(P(4, 64 * k, 64 * k + 64), "Z0", "Um", 1024 * k, (t, "m"))
        either(R("won"), P(4, 0, 128), AF.Sign, ALU.is_gt, 0.0)
        for k in range(4):
            gid = (t, "w", 1 if k % 2 else k)
            if k // 2 * 2 in CK:
                mm([(K[k], I, R("ck", 64 * k, 64 * k + 64))], gid)
            else:
                turn(K[k], obs[k] // 2, "S%d" % (obs[k] % 2), gid)
            mm([(K[k], I, R("PR", 64 * k, 64 * k + 64))], gid)
            if k % 2 == 0:
                wrap(K[k], "Zbig", "sg", 512 * k, gid)
        mm([(P(7, 0, 128), R("Iw"), R("won"))], (t, "w", 1))
        for i, k in enumerate(DO):
            tt(R("mi") if i == 3 else R("m%d" % (i % 2)), K[k], R("ns%d" % min(t, 1)) if i == 0 else R("m%d" % ((i + 1) % 2)), ALU.max)
        ts(R("mi2"), R("mi"), 8191, ALU.bitwise_and)
        cp(R("Dl"), R("mi2"))
        gat2("N1", 0, R("E"), "Dl")
        if t > 0:
            wrap(P(0, 0, 64), "Zpl", "N1", 0)
            cp(R("Dp"), P(0, 0, 64))
        gat2("N2", 0, R("N1"), "Dp" if t else "Dl")
        if REP:
            gat2("N1", 0, R("N2"), "Dp" if t else "Dl")
            gat2("E", gen, R("N1"), "Dp" if t else "Dl")
        else:
            wrap(P(1, 0, 64), "Zpl", "N2", 0)
            cp(R("D2l"), P(1, 0, 64))
            gat2("E", gen, R("N2"), "D2l")
        if t > 0:
            compose("E")
        if t < 2:
            wrap(P(0, 0, 64), "Za", "E", G0)
            ts(R("La"), P(0, 0, 64), float(-GH), ALU.add)
        if t == 1:
            mm([(P(4), R("Ir"), ones(512)), (P(4), R("Is"), R(So))] + [(P(4), R("Rw%d" % h), R("E", CU + h, PZ, 2)) for h in (0, 1)])
            tt(R(So), P(4), R(So), ALU.min)
            ts(R(Lo), R(So), float(OFF), ALU.add)

    for q in range(len(FIN) - 1):
        n0, n1 = FIN[q], FIN[q + 1]
        for par in (0, 1):
            for c in units(n0, n1, KF[q]):
                x = slot(c[1] - c[0])
                gat(x, R("E"), R("L%d" % par, *c))
                fold16(q, n0, c, lambda a: Z("Zpl", 2 * a + par), x, ("end", q))
        scl(R("outf", n0, n1), P(q, 0, n1 - n0), 1.0)
        dma("sp", T.ys[:, n0:n1], T.outf[:, n0:n1], [R("outf", n0, n1)], [])

    n = len(ops)
    users = [[] for _ in ops]
    for i, o in enumerate(ops):
        for j in set(o["deps"]) | set(o["order"]):
            users[j].append(i)
    rest = [0.0] * n
    for i in range(n - 1, -1, -1):
        rest[i] = ops[i]["cost"] + ops[i]["lat"] + HOP + max([rest[j] for j in users[i]] + [0.0]) + 1e-6 * (n - i)
    rest = [r + o["bias"] for r, o in zip(rest, ops)]
    left = [len(set(o["deps"]) | set(o["order"])) for o in ops]
    ready, free, end, est, line = [i for i in range(n) if left[i] == 0], {}, [0.0] * n, [0.0] * n, []
    while ready:
        t0, e = min((max(free.get(x, 0.0), est[i]), x) for i in ready for x in (("act", "dve") if ops[i]["eng"] == "any" else (ops[i]["eng"],)))
        mine_e = [i for i in ready if ops[i]["eng"] == e or (ops[i]["eng"] == "any" and e in ("act", "dve"))]
        key = {i: rest[i] + (OWN + QUICK * (ops[i]["cost"] < SHORT) if ops[i]["eng"] == e == "dve" else 0) for i in mine_e}
        i = max((i for i in mine_e if est[i] <= t0), key=key.get)
        soon = [j for j in mine_e if key[j] > key[i] and (ops[j]["eng"] == e or ops[j]["cost"] < SHORT) and est[j] - t0 < PATIENCE * ops[i]["cost"]]
        if soon:
            i = max(soon, key=key.get)
        o = ops[i]
        o["eng"] = e
        free[e] = max(t0, est[i]) + o["fast" if e == "dve" else "cost"]
        end[i] = free[e] + o["lat"]
        ready.remove(i)
        line.append(i)
        for j in users[i]:
            left[j] -= 1
            if i in ops[j]["deps"]:
                est[j] = max(est[j], end[i] + (0.0 if e == "pe" and ops[j]["eng"] == "pe" else HOP))
            if left[j] == 0:
                ready.append(j)

    place = {i: k for k, i in enumerate(line)}
    need, first, last = set(), {}, {}
    for i in line:
        o = ops[i]
        latest = {}
        for j in o["deps"]:
            x = ops[j]["eng"]
            if ops[j]["sem"] is None and not (x == "pe" and o["eng"] == "pe") and place[j] > place.get(latest.get(x), -1):
                latest[x] = j
        o["deps"] = [j for j in o["deps"] if ops[j]["sem"] is not None] + list(latest.values())
        need.update(latest.values())
        first.setdefault(o["gid"], i)
        last[o["gid"]] = i
    count, seen, final = {}, {}, {}
    for i in line:
        o = ops[i]
        e = o["eng"]
        if e != "ext":
            for j in o["deps"]:
                s, c = ops[j]["sem"], ops[j]["cnt"]
                if seen.get((e, s), 0) < c:
                    Q[e].wait_ge(T.sem[s], c)
                    seen[(e, s)] = c
            if e == "pe":
                gid = o["gid"]
                ins = o["fn"]((gid is None or first[gid] == i, gid is None or last[gid] == i))
            else:
                ins = o["fn"](e)
            if o["sem"] is None and i in need:
                count[e] = count.get(e, 0) + 1
                o["sem"], o["cnt"] = "c_" + e, count[e]
                ins.then_inc(T.sem[o["sem"]], 1)
            elif o["sem"] is not None and o["sem"][0] == "d":
                ins.then_inc(T.sem[o["sem"]], 16)
        if o["sem"] is not None:
            final[o["sem"]] = max(final.get(o["sem"], 0), o["cnt"])
    for s in sorted(final):
        if max([c for (e, s2), c in seen.items() if s2 == s] + [0]) < final[s]:
            g.sync.wait_ge(T.sem[s], final[s])
